import numpy as np, ml_dtypes
CORES = [3,7,11,15,131,135,139,143]
N = 8
import mx_ref
BF = ml_dtypes.bfloat16
def cols(t, e):
    v = np.concatenate([t.reshape(128, -1, 4), np.zeros((128, 1, 4), BF)], axis=1)
    return np.ascontiguousarray(v[:, e]).reshape(128, -1)
def decode(q):
    o = []
    for b in range(4):
        e = np.zeros((128, 128, 4), np.float32); e[np.arange(128), np.arange(128), b] = 1
        o.append(mx_ref.matmul(mx_ref.quantize(e.reshape(128, 512).astype(BF)), q))
    return np.stack(o, axis=2).reshape(128, -1)
def f(rng, *shape):
    return mx_ref.flush((rng.standard_normal(shape, dtype=np.float32) * np.exp2(rng.integers(-2, 3, shape[:-1] + (1,)))).astype(BF))
def wide(rng, *shape, cols=0):
    v = rng.standard_normal(shape, dtype=np.float32) * np.exp2(rng.integers(-12, 13, shape)).astype(np.float32)
    if cols: v *= np.repeat(np.exp2(rng.integers(-cols, cols + 1, shape[:-2] + (1, shape[-1] // 4))) * (rng.random(shape[:-2] + (1, shape[-1] // 4)) > 0.0625), 4, axis=-1).astype(np.float32)
    return mx_ref.flush(v.astype(BF))
T, K = 256, 32
def setup_inputs(rng):
    u = np.zeros((N, 128, 512), BF); u[:, :, :4] = f(rng, N, 128, 4)
    return {"gr": f(rng, N, 128, 4 * T), "u": u}
def raised(rng, chosen):
    d = setup_inputs(rng)
    for r in range(N):
        g = d["gr"][r].astype(np.float32).reshape(128, T, 4)
        sign = np.where(d["u"][r][:, :4].astype(np.float32) < 0, -1, 1).reshape(128, 1, 4) * rng.choice([-1, 1], K).reshape(1, K, 1)
        v = g * np.float32(2.0 ** -8)
        v[:, chosen[r]] = np.abs(g[:, chosen[r]]) * sign
        d["gr"][r] = mx_ref.flush(v.reshape(128, 4 * T).astype(BF))
    return d
def setup_inputs_same(rng):
    d = raised(rng, [rng.permutation(T)[:K]] * N)
    k = rng.permutation(np.concatenate([[12, -12, -11], rng.integers(-12, 13, N - 3)]))
    d["gr"] = mx_ref.flush((d["gr"].astype(np.float32) * np.exp2(k).astype(np.float32).reshape(N, 1, 1)).astype(BF))
    return d
def setup_inputs_apart(rng):
    p = rng.permutation(T)
    return raised(rng, [p[(r * K + np.arange(K)) % T] for r in range(N)])
def setup_inputs_ties(rng):
    d = setup_inputs(rng); n = T // 11
    for r in range(N):
        p = rng.permutation(T)[:11 * n]
        e = np.full(T, -1); e[p] = np.repeat(np.arange(n), 11)
        s = rng.choice([-1, 1], (n, 11)); s[:, 0] = 1; s[:, 1] = -1
        sign = np.ones(T, np.float32); sign[p] = s.reshape(-1)
        d["gr"][r] = (cols(d["gr"][r], e).astype(np.float32).reshape(128, T, 4) * sign.reshape(1, T, 1)).reshape(128, 4 * T).astype(BF)
    return d
def setup_inputs_few(rng):
    d = setup_inputs(rng); p = rng.permutation(N)
    d["u"][p[0]] = 0
    sign = rng.choice([-1, 1], (128, 1, 4))
    d["u"][p[1]][:, :4] = (sign * rng.uniform(1, 4, (128, 1, 4)) * 2.0 ** 28).reshape(128, 4).astype(BF)
    d["gr"][p[1]] = (sign * rng.choice([-1, 1], (1, T, 1)) * rng.uniform(1, 4, (128, T, 4)) * 2.0 ** 28).reshape(128, 4 * T).astype(BF)
    for r in p[2:2 + N // 2]:
        k = rng.permutation(T)[:rng.integers(1, K)]
        e = np.full(T, -1); e[k] = k
        d["gr"][r] = cols(d["gr"][r], e)
    return d
def setup_inputs_spread(rng):
    d = setup_inputs(rng); d["gr"] = wide(rng, N, 128, 4 * T, cols=8); return d
def check_inputs(d):
    return ["u"] if (d["u"][:, :, 4:].astype(np.float32) != 0).any() else []
def reference(gr, u):
    acc = np.zeros((128, T, 4), np.float32); nb = np.zeros((N, K), np.float32); sc = np.zeros((N, 1, K), np.float32)
    er = gr.astype(np.float32).reshape(N, 128, T, 4)
    for s in range(N):
        score = np.abs(mx_ref.matmul(mx_ref.quantize(u[s]), mx_ref.quantize(gr[s]))[0]) + np.float32(0.0)
        e = np.argsort(-score, kind="stable")[:K]
        v = decode(mx_ref.quantize(cols(gr[s], e))).reshape(128, K, 4)
        acc[:, e] = acc[:, e] + v
        er[s][:, e] = er[s][:, e] - v
        nb[s] = e
        sc[s, 0] = score[e]
    return {"acc": np.stack([acc.reshape(128, 4 * T)] * N), "er": er.reshape(N, 128, 4 * T), "nb": np.stack([nb] * N), "sc": sc}

@@ -1,0 +1,413 @@
+from concourse.bass import DstId, RemoteDMATransfer
+from concourse.mybir import dt, AluOpType, AxisListType, ActivationFunctionType
+
+K = 32
+TINY = 2.0 ** -120
+PRED = 1.0 - 2.0 ** -24
+HOLD = 2.0 ** 40
+OUT = -4096.0
+BB = 520
+
+F, B, I, U = "float32", "bfloat16", "int32", "uint16"
+C8, S8 = "float8_e4m3fn_x4", "uint8"
+SCRATCH = {
+    "grb": ("sbuf", [128, 1024], B), "ub": ("sbuf", [128, 16], B), "urep": ("sbuf", [128, 512], B), "hb": ("sbuf", [128, 512], B),
+    "eb": ("sbuf", [128, 528], B), "uo": ("sbuf", [128, 16], U),
+    "gq": ("sbuf", [128, 256], C8), "gs": ("sbuf", [128, 256], S8),
+    "uq": ("sbuf", [128, 128], C8), "us": ("sbuf", [128, 128], S8),
+    "eq": ("sbuf", [128, 512], C8), "es": ("sbuf", [128, 512], S8),
+    "qb": ("sbuf", [128, 160], C8), "qs": ("sbuf", [128, 160], S8),
+    "cb": ("sbuf", [128, 192], C8), "cs": ("sbuf", [128, 192], S8),
+    "lp": ("sbuf", [128, 16], U), "ll": ("sbuf", [128, 16], U), "ofo": ("sbuf", [128, 8], U),
+    "offp": ("sbuf", [128, 32], U), "offl": ("sbuf", [128, 64], U),
+    "ab": ("sbuf", [128, 256], F), "th": ("sbuf", [128, 256], F), "wt": ("sbuf", [128, 128], F),
+    "sth": ("sbuf", [128, 8], F),
+    "cmp": ("sbuf", [128, 512], B), "rks": ("sbuf", [128, 256], B), "rkf": ("sbuf", [128, 8], F),
+    "i32": ("sbuf", [128, 32], F), "coln": ("sbuf", [128, 2], B), "pi": ("sbuf", [128, 8], I), "pf": ("sbuf", [128, 16], F),
+    "ai": ("sbuf", [128, 32], F), "bi": ("sbuf", [128, 32], F), "k4": ("sbuf", [128, 32], F), "k8": ("sbuf", [128, 32], F),
+    "mk": ("sbuf", [128, 64], F), "r4": ("sbuf", [128, 32], F), "r16": ("sbuf", [128, 32], F),
+    "ce": ("sbuf", [128, 64], F), "cg": ("sbuf", [128, 64], F), "ch4": ("sbuf", [128, 256], B), "ch8": ("sbuf", [128, 256], B),
+    "vv": ("sbuf", [128, 64], F), "vt": ("sbuf", [128, 128], F), "q4": ("sbuf", [128, 8], F),
+    "xx": ("sbuf", [128, 64], F), "xt": ("sbuf", [128, 64], F), "sg4": ("sbuf", [128, 32], F), "sg16": ("sbuf", [128, 32], F),
+    "wv": ("sbuf", [128, 64], F), "wt2": ("sbuf", [128, 128], F), "wq": ("sbuf", [128, 8], F), "wx": ("sbuf", [128, 32], F),
+    "wy": ("sbuf", [128, 32], F), "zz": ("sbuf", [128, 16], F), "zt": ("sbuf", [128, 512], B),
+    "lf": ("sbuf", [128, 32], F), "nt": ("sbuf", [128, 32], F), "nu": ("sbuf", [128, 32], F),
+    "ent": ("sbuf", [128, 256], B), "m8": ("sbuf", [128, 2048], B), "rst": ("sbuf", [128, 2048], B), "mp": ("sbuf", [128, 2064], B),
+    "pr": ("sbuf", [128, 256], B), "hp": ("sbuf", [128, 256], B), "hl": ("sbuf", [128, 256], B),
+    "tv": ("sbuf", [128, 1040], F),
+    "acb": ("sbuf", [128, 1024], F), "erb": ("sbuf", [128, 1024], F), "vb": ("sbuf", [128, 1024], F),
+    "vo": ("sbuf", [128, 128], F), "te": ("sbuf", [128, 128], F),
+    "pa": ("psum", [128, 2048], F), "pb": ("psum", [128, 2048], F),
+}
+SEMAPHORES = ["v", "s", "t", "p", "dg1", "dg2", "du", "dl", "dh", "dm", "dsc", "dnb", "der", "dac", "l1", "c1", "s1", "c2", "s2", "sent", "left"]
+
+
+def rank_program(g, core, T, topo):
+    chip = topo.cores_of(core)
+    ranks = [c for c in T.cores if c in chip]
+    if not ranks:
+        return
+    others = [c for c in T.cores if c not in chip]
+    peers = [c for c in others if topo.die(c) == topo.die(core)]
+    helpers = [h for h in chip if h not in ranks and all(topo.may_write(h, c) for c in others)]
+    if core not in ranks and core not in helpers:
+        return
+
+    def pair(c):
+        return min(T.rank_of(d) for d in T.cores if d in topo.cores_of(c)) // 2
+
+    me = pair(core)
+
+    def slot(src, dst):
+        return src - (1 if src > dst else 0)
+
+    def ids(cores):
+        a = [topo.addr(c, core) for c in cores]
+        return [DstId(rid=r_, pnc=p_) for r_, p_ in a]
+
+    m2 = topo.mask(core, others[0])
+    for c in others:
+        m2 &= topo.mask(core, c)
+    n2 = bin(m2).count("1")
+
+    def hop2(dst, src, sem, local):
+        g.remote_dma_fused([RemoteDMATransfer(dst_ids=ids(peers), dma_engine_mask=m2, remote_sem=T.sem[sem], srcs=[src],
+                                              dsts=[dst(slot(me, pair(c))) for c in peers])], local_sem=T.sem[local])
+
+    if core in helpers:
+        g.wait_ge(T.sem.s1, sum(bin(topo.mask(c, core) & ~m2).count("1") for c in ranks))
+        hop2(lambda i: T.cs[:, 64 * i:64 * i + 64], T.qs[:, 0:64], "s2", "sent")
+        g.wait_ge(T.sem.sent, n2)
+        return
+
+    rank = T.rank_of(core)
+    partner = [c for c in ranks if c != core][0]
+    first = rank < T.rank_of(partner)
+    m1 = topo.mask(core, partner) & ~m2
+    n1 = bin(m1).count("1")
+
+    V, S, P, Y = g.vector, g.scalar, g.tensor, g.sync
+    Q = {"v": V, "s": S, "t": P, "p": g, "y": Y}
+    A, AF, X = AluOpType, ActivationFunctionType, AxisListType.X
+    cnt, seen = {"sent": 0, "left": 0}, {}
+
+    def done(sem, ins, n=1):
+        ins.then_inc(T.sem[sem], n)
+        cnt[sem] = cnt.get(sem, 0) + n
+        return (sem, cnt[sem])
+
+    def need(queue, *toks):
+        for sem, n in toks:
+            if seen.get((queue, sem), 0) < n:
+                Q[queue].wait_ge(T.sem[sem], n)
+                seen[(queue, sem)] = n
+
+    q0 = 0 if first else 32
+    own0 = 96 if first else 32
+    pair0 = 96 if first else 0
+    dec0 = 32 if first else 0
+    far_c = 0 if first else 128
+
+    d_u = done("du", S.dma_start(T.ub[:, 0:4], T.u[:, 0:4]), 16)
+    d_1 = done("dg1", Y.dma_start(T.grb[:, 0:512], T.gr[:, 0:512]), 16)
+    d_2 = done("dg2", Y.dma_start(T.grb[:, 512:1024], T.gr[:, 512:1024]), 16)
+
+    def iota(buf, pattern, base, cm):
+        return done("p", g.iota(buf, pattern, base, cm, allow_small_or_imprecise_dtypes=True))
+
+    done("v", V.memset(T.zz[:], 0.0))
+    k_wt = done("v", V.memset(T.wt[:], PRED))
+    k_eb = done("v", V.memset(T.eb[:], 1.0))
+    k_p = done("p", g.iota(T.pi[:, 0:1], [[1, 1]], 0, 1))
+    k_i = iota(T.i32[:], [[1, 32]], 0, 0)
+    need("p", k_wt)
+    k_wt = done("p", g.affine_select(T.wt[:], T.wt[:], [[-1, 128]], A.is_gt, 1.0, 0, 1))
+    need("p", k_eb)
+    k_eb = done("p", g.affine_select(T.eb[:, 0:516], T.eb[:, 0:516], [[-1, 516]], A.is_equal, 0.0, 3, 4))
+    iota(T.ai[:], [[0, 2], [1, 4], [0, 4]], 0, 0)
+    k_b = iota(T.bi[:], [[0, 2], [1, 16]], 0, 0)
+    k_c = iota(T.coln[:], [[128, 2]], 0, 1)
+    iota(T.k4[:], [[0, 8], [1, 4]], 0, 0)
+    k_kk = iota(T.k8[:], [[0, 4], [1, 8]], 0, 0)
+    need("v", k_p)
+    done("v", V.tensor_scalar(T.pi[:, 1:2], T.pi[:, 0:1], 3, None, A.bitwise_and))
+    done("v", V.tensor_scalar(T.pi[:, 2:3], T.pi[:, 0:1], 2, 3, A.logical_shift_right, A.bitwise_and))
+    done("v", V.tensor_scalar(T.pi[:, 3:4], T.pi[:, 0:1], 15, None, A.bitwise_and))
+    done("v", V.tensor_scalar(T.pi[:, 4:5], T.pi[:, 0:1], 1, None, A.bitwise_and))
+    done("v", V.tensor_scalar(T.pi[:, 5:6], T.pi[:, 0:1], 1, 7, A.logical_shift_right, A.bitwise_and))
+    k = done("v", V.tensor_scalar(T.pi[:, 6:7], T.pi[:, 0:1], 1, 1, A.logical_shift_right, A.bitwise_and))
+    done("v", V.memset(T.r4[:], 1.0))
+    need("v", k)
+    k = done("v", V.tensor_copy(T.pf[:, 0:6], T.pi[:, 1:7]))
+    p4, pq4, p16, p1, pq8, ph = [T.pf[:, i:i + 1] for i in range(6)]
+    k2 = done("v", V.memset(T.r16[:], 1.0))
+    need("v", k)
+    k_uo = done("v", V.tensor_scalar(T.uo[:], T.zz[:], p4, None, A.add))
+    done("v", V.memset(T.r4[:, 0:32:4], 0.0))
+    need("v", k2)
+    done("v", V.memset(T.r16[:, 0:32:16], 0.0))
+    k_zt = done("v", V.memset(T.zt[:], 0.0))
+    need("y", k_zt)
+    d_h = done("dh", Y.dma_start(T.hb[:], T.zt[:]), 16)
+    for a in range(4):
+        d_m = done("dm", Y.dma_start(T.m8[:, 512 * a:512 * a + 512], T.zt[:]), 16)
+    need("s", k_i)
+    for s in range(8):
+        a_en = done("s", S.activation(T.ent[:, 32 * s:32 * s + 32], T.i32[:], AF.Copy, bias=float(32 * s + 1)))
+
+    need("s", d_u, k_uo)
+    a_u = done("s", S.activation(T.urep[:, 256:512], T.ub[:, 0:4].indirect(T.uo[:, 0:16]), AF.Copy))
+    for z in (T.tv[:, 0:2], T.tv[:, 514:BB + 2], T.mp[:, 0:1], T.lf[:], T.wx[:]):
+        done("s", S.activation(z, T.i32[:, 0:z.shape[1]], AF.Copy, scale=0.0))
+    need("v", d_u, k_uo)
+    k = done("v", V.tensor_copy(T.urep[:, 0:256], T.ub[:, 0:4].indirect(T.uo[:, 0:16])))
+    need("v", k, a_u)
+    k_u = done("v", V.quantize_mx(T.uq[:], T.us[:], T.urep[:]))
+
+    def tile_e(b):
+        need("v", k_eb)
+        return done("v", V.quantize_mx(T.eq[:, 128 * b:128 * b + 128], T.es[:, 128 * b:128 * b + 128], T.eb[:, 3 - b:515 - b]))
+
+    a_c, a_f = [], []
+    for h in range(2):
+        j = 128 * h
+        need("v", (d_1, d_2)[h])
+        k_g = done("v", V.quantize_mx(T.gq[:, j:j + 128], T.gs[:, j:j + 128], T.grb[:, 512 * h:512 * h + 512]))
+        need("t", k_u, k_g)
+        t_c = done("t", P.matmul_mx(T.pa[:, 1024 * h:1024 * h + 128], T.gq[:, j:j + 128], T.gs[:, j:j + 128], T.uq[:], T.us[:], True, True))
+        t_f = done("t", P.matmul_mx(T.pa[:, 1024 * h + 512:1024 * h + 640], T.uq[:], T.us[:], T.gq[:, j:j + 128], T.gs[:, j:j + 128], True, True))
+        need("s", t_c)
+        a_c.append(done("s", S.activation(T.sth[:, h:h + 1], T.pa[:, 1024 * h:1024 * h + 1], AF.Abs, bias=TINY)))
+        need("s", t_f)
+        a_f.append(done("s", S.activation(T.ab[:, j:j + 128], T.pa[:, 1024 * h + 512:1024 * h + 640], AF.Abs, bias=TINY)))
+        k_e = tile_e(h)
+
+    s0, s1 = T.sth[:, 0:1], T.sth[:, 1:2]
+    need("s", k_wt, a_c[1])
+    a_t = done("s", S.activation(T.th[:, 128:256], T.wt[:], AF.Copy, scale=s1))
+    need("v", a_c[0], k_wt)
+    k_d = done("v", V.tensor_scalar(T.th[:, 0:128], T.wt[:], s0, None, A.mult))
+    k_e = tile_e(2)
+    need("v", a_f[0], k_d)
+    done("v", V.tensor_tensor(T.cmp[:, 0:128], T.ab[:, 0:128], T.th[:, 0:128], A.is_gt))
+    need("v", a_c[1])
+    done("v", V.tensor_scalar(T.cmp[:, 256:384], T.ab[:, 0:128], s1, None, A.is_ge))
+    need("v", a_f[1])
+    k0 = done("v", V.tensor_scalar(T.cmp[:, 128:256], T.ab[:, 128:256], s0, None, A.is_gt))
+    need("v", a_t)
+    k1 = done("v", V.tensor_tensor(T.cmp[:, 384:512], T.ab[:, 128:256], T.th[:, 128:256], A.is_gt))
+    need("v", k0)
+    k0 = done("v", V.tensor_tensor_scan(T.rks[:, 0:128], T.cmp[:, 0:128], T.cmp[:, 128:256], 0.0, A.add, A.add))
+    need("v", k1)
+    k1 = done("v", V.tensor_tensor_scan(T.rks[:, 128:256], T.cmp[:, 256:384], T.cmp[:, 384:512], 0.0, A.add, A.add))
+    rk = [T.rks[:, 127:128], T.rks[:, 255:256]]
+
+    def ones(h):
+        return done("s", S.activation(T.rst[:, 1024 * h:1024 * h + 1024], T.grb[:], AF.Copy, scale=0.0, bias=1.0))
+
+    need("s", d_1, d_2)
+    ones(0)
+
+    need("v", k_c, k0)
+    done("v", V.tensor_scalar(T.vv[:, 0:32], T.i32[:], rk[0], T.coln[:, 0:1], A.is_equal, A.mult))
+    need("v", k1)
+    k = done("v", V.tensor_scalar(T.vv[:, 32:64], T.i32[:], rk[1], T.coln[:, 1:2], A.is_equal, A.mult))
+    need("v", k_b)
+    done("v", V.tensor_scalar(T.mk[:, 0:32], T.ai[:], p4, OUT, A.not_equal, A.mult))
+    need("v", k)
+    for a in range(2):
+        k = done("v", V.transpose(T.vt[0:64, 64 * a:64 * a + 64], T.vv[64 * a:64 * a + 64, :]))
+    done("v", V.tensor_scalar(T.mk[:, 32:64], T.bi[:], p16, OUT, A.not_equal, A.mult))
+    need("v", k)
+    k = done("v", V.tensor_reduce(T.q4[0:64, 0:1], T.vt[0:64, :], X, A.add))
+    need("v", k)
+    for a in range(4):
+        k = done("v", V.tensor_scalar(T.xx[32 * a:32 * a + 32, :], T.mk[0:32, :], T.q4[0:32, 0:1], T.q4[32:64, 0:1], A.add, A.add))
+    need("v", k)
+    k = done("v", V.transpose(T.xt[:], T.xx[:]))
+    need("v", k)
+    k4 = done("v", V.tensor_tensor_scan(T.sg4[:], T.r4[:], T.xt[:, 0:32], 0.0, A.mult, A.max))
+    k8 = done("v", V.tensor_tensor_scan(T.sg16[:], T.r16[:], T.xt[:, 32:64], 0.0, A.mult, A.max))
+    need("v", k4)
+    k_o = done("v", V.tensor_scalar(T.ofo[:], T.sg4[:, 3:32:4], 4.0, p4, A.mult, A.add))
+    need("v", k8)
+    k_lp = done("v", V.tensor_scalar(T.lp[:, 0:2], T.sg16[:, 15:32:16], 8.0, float(rank), A.mult, A.add))
+    h0 = 4 * (own0 - q0)
+    need("s", k_o, d_h)
+    a_h = done("s", S.activation(T.hb[:, h0 + 64:h0 + 128], T.grb[:, 0:1024].indirect(T.ofo[:, 4:8]), AF.Copy))
+    need("v", k_o, d_h)
+    k = done("v", V.tensor_copy(T.hb[:, h0:h0 + 64], T.grb[:, 0:1024].indirect(T.ofo[:, 0:4])))
+    need("v", k, a_h)
+    k_q = done("v", V.quantize_mx(T.qb[:, q0:q0 + 128], T.qs[:, q0:q0 + 128], T.hb[:]))
+    a_e = done("s", S.activation(T.erb[:], T.grb[:], AF.Copy))
+    mine = T.ll[:, 2 * rank:2 * rank + 2]
+    need("y", k_lp)
+    d_l = done("dl", Y.dma_start(mine, T.lp[:, 0:2]), 16)
+
+    b8 = dt.uint8
+    LL, C1, S1 = ("l1", n1 + len(others) * n2), ("c1", n1), ("s1", n1)
+    C2, S2 = ("c2", 3 * n2), ("s2", 3 * n2)
+    need("p", k_lp)
+    g.remote_dma_fused([
+        RemoteDMATransfer(dst_ids=ids(others), dma_engine_mask=m2, remote_sem=T.sem.l1, srcs=[T.lp[:, 0:2]], dsts=[mine for c in others]),
+        RemoteDMATransfer(dst_ids=ids([partner]), dma_engine_mask=m1, remote_sem=T.sem.l1, srcs=[T.lp[:, 0:2]], dsts=[mine]),
+    ], local_sem=T.sem.sent)
+    need("p", k_q)
+    rid, pid = topo.addr(partner, core)
+    g.remote_dma(out_ap=T.qb[:, far_c:far_c + 32].bitcast(b8), in_ap=T.qb[:, own0:own0 + 32].bitcast(b8), remote_sem=T.sem.c1,
+                 local_sem=T.sem.sent, pid=pid, routing_id=rid, dma_engine_mask=m1)
+    hs = 0 if first else 32
+    g.remote_dma_fused([RemoteDMATransfer(dst_ids=ids(helpers + [partner]), dma_engine_mask=m1, remote_sem=T.sem.s1,
+                                          srcs=[T.qs[:, own0:own0 + 32]],
+                                          dsts=[T.qs[:, hs:hs + 32] for h in helpers] + [T.qs[:, far_c:far_c + 32]])], local_sem=T.sem.sent)
+    cnt["sent"] += 3 * n1 + n2
+    need("p", C1)
+    hop2(lambda i: T.cb[:, 64 * i:64 * i + 64].bitcast(b8), T.qb[:, pair0:pair0 + 64].bitcast(b8), "c2", "left")
+    cnt["left"] += n2
+
+    k_e = tile_e(3)
+    f4, f8, e4, e8, x4, x8, pl, ps = [T.pf[:, 6 + i:7 + i] for i in range(8)]
+    need("v", k_kk)
+    done("v", V.tensor_scalar(f4, pq4, 1.0, None, A.add))
+    k = done("v", V.tensor_scalar(f8, pq8, 1.0, None, A.add))
+    done("v", V.tensor_scalar(e4, pq4, 3.0, 2.0, A.is_equal, A.mult))
+    c = done("v", V.tensor_scalar(e8, pq8, 7.0, 2.0, A.is_equal, A.mult))
+    done("v", V.tensor_scalar(pl, ph, float(BB), p1, A.mult, A.add))
+    done("v", V.tensor_scalar(ps, pq8, -0.125, None, A.mult))
+    need("v", k)
+    done("v", V.tensor_scalar(T.ce[:, 0:32], T.k8[:], f8, HOLD, A.is_equal, A.mult))
+    done("v", V.tensor_scalar(T.ce[:, 32:64], T.k4[:], f4, HOLD, A.is_equal, A.mult))
+    done("v", V.tensor_scalar(T.cg[:, 0:32], T.k8[:], f8, None, A.is_gt))
+    k = done("v", V.tensor_scalar(T.cg[:, 32:64], T.k4[:], f4, None, A.is_gt))
+    need("v", c)
+    done("v", V.tensor_scalar(x4, e4, 2.0 / HOLD, None, A.max))
+    done("v", V.tensor_scalar(x8, e8, 2.0 / HOLD, None, A.max))
+    need("v", k)
+    done("v", V.tensor_tensor(T.ch8[:, 0:32], T.ce[:, 0:32], T.cg[:, 0:32], A.max))
+    a_ch = done("v", V.tensor_tensor(T.ch4[:, 0:32], T.ce[:, 32:64], T.cg[:, 32:64], A.max))
+
+    def decode(ps, n, codes, scales):
+        return [done("t", P.matmul_mx(ps[:, 512 * b:512 * b + n], T.eq[:, 128 * b:128 * b + 128], T.es[:, 128 * b:128 * b + 128],
+                                      codes, scales, True, True)) for b in range(4)]
+
+    def empty(q, tok, dst, src):
+        need(q, tok)
+        if q == "s":
+            return done("s", S.activation(dst, src, AF.Copy))
+        return done("v", V.tensor_copy(dst, src))
+
+    need("t", k_e, a_f[1], k_q)
+    td = decode(T.pa, 128, T.qb[:, q0:q0 + 128], T.qs[:, q0:q0 + 128])
+    vo = [empty("s" if b % 2 else "v", td[b], T.vo[:, b:128:4], T.pa[:, 512 * b + own0 - q0:512 * b + own0 - q0 + 32]) for b in range(4)]
+    need("s", k1)
+    for h in range(2):
+        a_rk = done("s", S.activation(T.rkf[:, h:h + 1], rk[h], AF.Copy))
+    a_r = ones(1)
+    need("v", a_e, *vo)
+    k = done("v", V.tensor_tensor(T.te[:], T.erb[:, 0:1024].indirect(T.ofo[:, 0:8]), T.vo[:], A.subtract))
+    need("v", a_rk)
+    done("v", V.tensor_scalar(T.wv[:, 0:32], T.i32[:], T.rkf[:, 0:1], T.sth[:, 0:1], A.is_equal, A.mult))
+    w = done("v", V.tensor_scalar(T.wv[:, 32:64], T.i32[:], T.rkf[:, 1:2], T.sth[:, 1:2], A.is_equal, A.mult))
+    need("v", k)
+    k_er = done("v", V.tensor_copy(T.erb[:, 0:1024].indirect(T.ofo[:, 0:8]), T.te[:]))
+    need("y", k_er, ("left", n2))
+    d_er = done("der", Y.dma_start(T.er[:], T.erb[:]), 16)
+    need("v", w)
+    for a in range(2):
+        w = done("v", V.transpose(T.wt2[0:64, 64 * a:64 * a + 64], T.wv[64 * a:64 * a + 64, :]))
+    need("v", a_r)
+    k_r = done("v", V.memset(T.rst[:, 0:2048:8], 0.0))
+    need("v", w)
+    w = done("v", V.tensor_reduce(T.wq[0:64, 0:1], T.wt2[0:64, :], X, A.add))
+    need("v", w)
+    w = done("v", V.tensor_scalar(T.wx[0:32, 0:1], T.wq[0:32, 0:1], T.wq[32:64, 0:1], TINY, A.add, A.subtract))
+    need("v", w)
+    w = done("v", V.transpose(T.wy[0:32, :], T.wx[0:32, :]))
+    need("y", w)
+    d_sc = done("dsc", Y.dma_start(T.sc[:], T.wy[0:1, :]), 16)
+    for n in (32, 64, 128):
+        need("s", a_ch)
+        done("s", S.activation(T.ch8[:, n:2 * n], T.ch8[:, 0:n], AF.Copy))
+        a_ch = done("s", S.activation(T.ch4[:, n:2 * n], T.ch4[:, 0:n], AF.Copy))
+
+    need("t", C1, S1, *vo)
+    td = decode(T.pa, 128, T.qb[:, dec0:dec0 + 128], T.qs[:, dec0:dec0 + 128])
+    for b in range(4):
+        h, i, c0 = b // 2, b % 2, 512 * b + pair0 - dec0
+        if me == 0:
+            empty("s", td[b], T.tv[:, BB * h + 2 + i:BB * h + 66:2], T.pa[:, c0:c0 + 32])
+            a_p = empty("s", td[b], T.vb[:, 512 * h + 64 + i:512 * h + 128:2], T.pa[:, c0 + 32:c0 + 64])
+        else:
+            a_p = empty("s", td[b], T.vb[:, 512 * h + i:512 * h + 128:2], T.pa[:, c0:c0 + 64])
+
+    need("v", LL, d_l, a_en, d_m, a_ch, k_r)
+    k = done("v", V.tensor_copy(T.m8[:, 0:2048].indirect(T.ll[:, 0:16]), T.ent[:]))
+    n = done("v", V.tensor_copy(T.lf[0:32, 0:16], T.ll[0:32, 0:16]))
+    need("v", k)
+    k = done("v", V.tensor_tensor_scan(T.mp[:, 1:2049], T.rst[:], T.m8[:], 0.0, A.mult, A.max))
+    need("v", n)
+    n = done("v", V.transpose(T.nt[0:32, :], T.lf[0:32, :]))
+    need("v", k)
+    k = done("v", V.tensor_copy(T.pr[:, 0:224], T.mp[:, 0:2048].indirect(T.ll[:, 2:16])))
+    need("v", n)
+    k_nb = done("v", V.tensor_scalar(T.nu[0:32, :], T.nt[0:32, :], 0.125, T.pf[0:32, 13:14], A.mult, A.add))
+    need("v", k)
+    k = done("v", V.tensor_tensor_scan(T.hp[:, 0:224], T.ch8[:, 0:224], T.pr[:, 0:224], 0.0, A.mult, A.add))
+    need("v", k)
+    k_op = done("v", V.tensor_scalar(T.offp[:, 0:28], T.hp[:, 7:224:8], x8, p1, A.mult, A.add))
+    need("y", k_nb)
+    d_nb = done("dnb", Y.dma_start(T.nb[:], T.nu[0:16, 0:16]), 16)
+
+    need("t", C2, S2)
+    td = decode(T.pb, 192, T.cb[:], T.cs[:])
+    got = [[], []]
+
+    def landed(b, part):
+        h, i, q, n = b // 2, b % 2, "s" if b % 2 else "v", 0 if me == 0 else 32
+        if part == 0 and n:
+            got[h].append(empty(q, td[b], T.tv[:, BB * h + 2 + i:BB * h + 66:2], T.pb[:, 512 * b:512 * b + 32]))
+        if part == 1:
+            got[h].append(empty(q, td[b], T.vb[:, 512 * h + 128 + 2 * n + i:512 * h + 512:2], T.pb[:, 512 * b + n:512 * b + 192]))
+
+    for b in (0, 1, 3):
+        landed(b, 0)
+        landed(b, 1)
+
+    last = [None, None]
+
+    def add(h, s):
+        m = s // 2
+        at = (s % 2) if m == me else 2 + 2 * slot(m, me) + s % 2
+        need("v", k_op, a_p, *got[h])
+        if last[h]:
+            need("v", last[h])
+        last[h] = done("v", V.tensor_tensor(T.tv[:, BB * h + 2 + 64 * s:BB * h + 66 + 64 * s],
+                                            T.tv[:, BB * h:BB * h + 2 + 64 * s].indirect(T.offp[:, 4 * s - 4:4 * s]),
+                                            T.vb[:, 512 * h + 64 * at:512 * h + 64 * at + 64], A.add))
+
+    for s in range(1, 10):
+        if s < 8:
+            add(0, s)
+        if s < 3:
+            landed(2, s - 1)
+        else:
+            add(1, s - 2)
+        if s == 7:
+            k_hl = done("v", V.tensor_tensor_scan(T.hl[:], T.ch4[:], T.mp[:, 8:2049:8], 0.0, A.mult, A.add))
+        if s == 8:
+            need("v", k_hl)
+            k_ol = done("v", V.tensor_scalar(T.offl[:], T.hl[:, 3:256:4], x4, pl, A.mult, A.add))
+
+    need("v", k_ol, *last)
+    need("s", k_ol, *last)
+    win, parts = T.tv[:, 0:BB + 514], []
+    for i in range(2):
+        parts.append((256 * i, done("v", V.tensor_copy(T.acb[:, 256 * i:256 * i + 256], win.indirect(T.offl[:, 16 * i:16 * i + 16])))))
+        parts.append((512 + 256 * i, done("s", S.activation(T.acb[:, 512 + 256 * i:768 + 256 * i], win.indirect(T.offl[:, 32 + 16 * i:48 + 16 * i]), AF.Copy))))
+    for c, tok in parts:
+        q = "s" if tok == parts[-1][1] else "y"
+        need(q, tok)
+        d_ac = done("dac", Q[q].dma_start(T.acc[:, c:c + 256], T.acb[:, c:c + 256]), 16)
+
+    need("p", d_u, d_1, d_2, d_h, d_m, d_l, d_er, d_nb, d_ac, d_sc, LL, C2, S2)
+    need("p", *[(x, cnt[x]) for x in ("v", "s", "t", "p", "sent", "left")])

@@ -4,9 +4,11 @@ from concourse.mybir import dt, AluOpType, AxisListType, ActivationFunctionType
 K = 32
 TINY = 2.0 ** -120
 PRED = 1.0 - 2.0 ** -24
-HOLD = 2.0 ** 40
+HOLD = 2.0 ** 14
+ROUND = 1.5 * 2.0 ** 23
 OUT = -4096.0
 BB = 520
+PIECES = (0, 256, 640, 1024)
 
 F, B, I, U = "float32", "bfloat16", "int32", "uint16"
 C8, S8 = "float8_e4m3fn_x4", "uint8"
@@ -24,9 +26,9 @@ SCRATCH = {
     "sth": ("sbuf", [128, 8], F),
     "cmp": ("sbuf", [128, 512], B), "rks": ("sbuf", [128, 256], B), "rkf": ("sbuf", [128, 8], F),
     "i32": ("sbuf", [128, 32], F), "coln": ("sbuf", [128, 2], B), "pi": ("sbuf", [128, 8], I), "pf": ("sbuf", [128, 16], F),
-    "ai": ("sbuf", [128, 32], F), "bi": ("sbuf", [128, 32], F), "k4": ("sbuf", [128, 32], F), "k8": ("sbuf", [128, 32], F),
+    "ai": ("sbuf", [128, 32], F), "bi": ("sbuf", [128, 32], F), "k4": ("sbuf", [128, 256], B), "k8": ("sbuf", [128, 256], B),
     "mk": ("sbuf", [128, 64], F), "r4": ("sbuf", [128, 32], F), "r16": ("sbuf", [128, 32], F),
-    "ce": ("sbuf", [128, 64], F), "cg": ("sbuf", [128, 64], F), "ch4": ("sbuf", [128, 256], B), "ch8": ("sbuf", [128, 256], B),
+    "y48": ("sbuf", [128, 16], F), "ch4": ("sbuf", [128, 256], B), "ch8": ("sbuf", [128, 256], B),
     "vv": ("sbuf", [128, 64], F), "vt": ("sbuf", [128, 128], F), "q4": ("sbuf", [128, 8], F),
     "xx": ("sbuf", [128, 64], F), "xt": ("sbuf", [128, 64], F), "sg4": ("sbuf", [128, 32], F), "sg16": ("sbuf", [128, 32], F),
     "wv": ("sbuf", [128, 64], F), "wt2": ("sbuf", [128, 128], F), "wq": ("sbuf", [128, 8], F), "wx": ("sbuf", [128, 32], F),
@@ -39,7 +41,8 @@ SCRATCH = {
     "vo": ("sbuf", [128, 128], F), "te": ("sbuf", [128, 128], F),
     "pa": ("psum", [128, 2048], F), "pb": ("psum", [128, 2048], F),
 }
-SEMAPHORES = ["v", "s", "t", "p", "dg1", "dg2", "du", "dl", "dh", "dm", "dsc", "dnb", "der", "dac", "l1", "c1", "s1", "c2", "s2", "sent", "left"]
+SEMAPHORES = ["v", "s", "t", "p", "dg1", "dg2", "du", "dl", "dh", "dm", "dsc", "dnb", "der", "dac", "l1", "l2", "c1", "s1", "c2", "s2",
+              "sent", "left"]
 
 
 def rank_program(g, core, T, topo):
@@ -85,6 +88,8 @@ def rank_program(g, core, T, topo):
     first = rank < T.rank_of(partner)
     m1 = topo.mask(core, partner) & ~m2
     n1 = bin(m1).count("1")
+    order = sorted(range(len(T.cores)), key=lambda s: (topo.die(T.cores[s]) != topo.die(T.cores[0]), s))
+    at_l = order.index(rank)
 
     V, S, P, Y = g.vector, g.scalar, g.tensor, g.sync
     Q = {"v": V, "s": S, "t": P, "p": g, "y": Y}
@@ -115,20 +120,22 @@ def rank_program(g, core, T, topo):
     def iota(buf, pattern, base, cm):
         return done("p", g.iota(buf, pattern, base, cm, allow_small_or_imprecise_dtypes=True))
 
+    k = done("v", V.memset(T.eb[:], 0.0))
     done("v", V.memset(T.zz[:], 0.0))
     k_wt = done("v", V.memset(T.wt[:], PRED))
-    k_eb = done("v", V.memset(T.eb[:], 1.0))
+    need("v", k)
+    e3 = T.eb[:, 3:515:4]
+    k_eb = done("v", V.memset(e3, 1.0))
     k_p = done("p", g.iota(T.pi[:, 0:1], [[1, 1]], 0, 1))
     k_i = iota(T.i32[:], [[1, 32]], 0, 0)
-    need("p", k_wt)
-    k_wt = done("p", g.affine_select(T.wt[:], T.wt[:], [[-1, 128]], A.is_gt, 1.0, 0, 1))
     need("p", k_eb)
-    k_eb = done("p", g.affine_select(T.eb[:, 0:516], T.eb[:, 0:516], [[-1, 516]], A.is_equal, 0.0, 3, 4))
+    k_eb = done("p", g.affine_select(e3, e3, [[-1, 128]], A.is_equal, 0.0, 0, 1))
+    k_wt = done("p", g.affine_select(T.wt[:], T.wt[:], [[-1, 128]], A.is_gt, 1.0, 0, 1))
+    k_8 = iota(T.k8[:], [[0, 32], [1, 8]], 0, 0)
     iota(T.ai[:], [[0, 2], [1, 4], [0, 4]], 0, 0)
     k_b = iota(T.bi[:], [[0, 2], [1, 16]], 0, 0)
     k_c = iota(T.coln[:], [[128, 2]], 0, 1)
-    iota(T.k4[:], [[0, 8], [1, 4]], 0, 0)
-    k_kk = iota(T.k8[:], [[0, 4], [1, 8]], 0, 0)
+    k_4 = iota(T.k4[:], [[0, 64], [1, 4]], 0, 0)
     need("v", k_p)
     done("v", V.tensor_scalar(T.pi[:, 1:2], T.pi[:, 0:1], 3, None, A.bitwise_and))
     done("v", V.tensor_scalar(T.pi[:, 2:3], T.pi[:, 0:1], 2, 3, A.logical_shift_right, A.bitwise_and))
@@ -136,33 +143,28 @@ def rank_program(g, core, T, topo):
     done("v", V.tensor_scalar(T.pi[:, 4:5], T.pi[:, 0:1], 1, None, A.bitwise_and))
     done("v", V.tensor_scalar(T.pi[:, 5:6], T.pi[:, 0:1], 1, 7, A.logical_shift_right, A.bitwise_and))
     k = done("v", V.tensor_scalar(T.pi[:, 6:7], T.pi[:, 0:1], 1, 1, A.logical_shift_right, A.bitwise_and))
-    done("v", V.memset(T.r4[:], 1.0))
+    k_zt = done("v", V.memset(T.zt[:], 0.0))
     need("v", k)
     k = done("v", V.tensor_copy(T.pf[:, 0:6], T.pi[:, 1:7]))
     p4, pq4, p16, p1, pq8, ph = [T.pf[:, i:i + 1] for i in range(6)]
-    k2 = done("v", V.memset(T.r16[:], 1.0))
+    x4, x8, pl = [T.pf[:, 6 + i:7 + i] for i in range(3)]
     need("v", k)
     k_uo = done("v", V.tensor_scalar(T.uo[:], T.zz[:], p4, None, A.add))
-    done("v", V.memset(T.r4[:, 0:32:4], 0.0))
-    need("v", k2)
-    done("v", V.memset(T.r16[:, 0:32:16], 0.0))
-    k_zt = done("v", V.memset(T.zt[:], 0.0))
+    done("v", V.tensor_scalar(pl, ph, float(BB), p1, A.mult, A.add))
     need("y", k_zt)
     d_h = done("dh", Y.dma_start(T.hb[:], T.zt[:]), 16)
     for a in range(4):
         d_m = done("dm", Y.dma_start(T.m8[:, 512 * a:512 * a + 512], T.zt[:]), 16)
     need("s", k_i)
-    for s in range(8):
-        a_en = done("s", S.activation(T.ent[:, 32 * s:32 * s + 32], T.i32[:], AF.Copy, bias=float(32 * s + 1)))
+    for a, s in enumerate(order):
+        a_en = done("s", S.activation(T.ent[:, 32 * a:32 * a + 32], T.i32[:], AF.Copy, scale=2.0, bias=float(64 * s + 2)))
 
     need("s", d_u, k_uo)
     a_u = done("s", S.activation(T.urep[:, 256:512], T.ub[:, 0:4].indirect(T.uo[:, 0:16]), AF.Copy))
     for z in (T.tv[:, 0:2], T.tv[:, 514:BB + 2], T.mp[:, 0:1], T.lf[:], T.wx[:]):
         done("s", S.activation(z, T.i32[:, 0:z.shape[1]], AF.Copy, scale=0.0))
     need("v", d_u, k_uo)
-    k = done("v", V.tensor_copy(T.urep[:, 0:256], T.ub[:, 0:4].indirect(T.uo[:, 0:16])))
-    need("v", k, a_u)
-    k_u = done("v", V.quantize_mx(T.uq[:], T.us[:], T.urep[:]))
+    k_u = done("v", V.tensor_copy(T.urep[:, 0:256], T.ub[:, 0:4].indirect(T.uo[:, 0:16])))
 
     def tile_e(b):
         need("v", k_eb)
@@ -173,6 +175,9 @@ def rank_program(g, core, T, topo):
         j = 128 * h
         need("v", (d_1, d_2)[h])
         k_g = done("v", V.quantize_mx(T.gq[:, j:j + 128], T.gs[:, j:j + 128], T.grb[:, 512 * h:512 * h + 512]))
+        if h == 0:
+            need("v", k_u, a_u)
+            k_u = done("v", V.quantize_mx(T.uq[:], T.us[:], T.urep[:]))
         need("t", k_u, k_g)
         t_c = done("t", P.matmul_mx(T.pa[:, 1024 * h:1024 * h + 128], T.gq[:, j:j + 128], T.gs[:, j:j + 128], T.uq[:], T.us[:], True, True))
         t_f = done("t", P.matmul_mx(T.pa[:, 1024 * h + 512:1024 * h + 640], T.uq[:], T.us[:], T.gq[:, j:j + 128], T.gs[:, j:j + 128], True, True))
@@ -180,14 +185,14 @@ def rank_program(g, core, T, topo):
         a_c.append(done("s", S.activation(T.sth[:, h:h + 1], T.pa[:, 1024 * h:1024 * h + 1], AF.Abs, bias=TINY)))
         need("s", t_f)
         a_f.append(done("s", S.activation(T.ab[:, j:j + 128], T.pa[:, 1024 * h + 512:1024 * h + 640], AF.Abs, bias=TINY)))
-        k_e = tile_e(h)
+        if h == 0:
+            tile_e(0)
 
     s0, s1 = T.sth[:, 0:1], T.sth[:, 1:2]
     need("s", k_wt, a_c[1])
     a_t = done("s", S.activation(T.th[:, 128:256], T.wt[:], AF.Copy, scale=s1))
     need("v", a_c[0], k_wt)
     k_d = done("v", V.tensor_scalar(T.th[:, 0:128], T.wt[:], s0, None, A.mult))
-    k_e = tile_e(2)
     need("v", a_f[0], k_d)
     done("v", V.tensor_tensor(T.cmp[:, 0:128], T.ab[:, 0:128], T.th[:, 0:128], A.is_gt))
     need("v", a_c[1])
@@ -202,17 +207,16 @@ def rank_program(g, core, T, topo):
     k1 = done("v", V.tensor_tensor_scan(T.rks[:, 128:256], T.cmp[:, 256:384], T.cmp[:, 384:512], 0.0, A.add, A.add))
     rk = [T.rks[:, 127:128], T.rks[:, 255:256]]
 
-    def ones(h):
-        return done("s", S.activation(T.rst[:, 1024 * h:1024 * h + 1024], T.grb[:], AF.Copy, scale=0.0, bias=1.0))
+    def resets(a, b):
+        need("s", k_8)
+        return [done("s", S.activation(T.rst[:, 256 * i:256 * i + 256], T.k8[:], AF.Sign)) for i in range(a, b)][-1]
 
-    need("s", d_1, d_2)
-    ones(0)
+    resets(0, 5)
 
     need("v", k_c, k0)
     done("v", V.tensor_scalar(T.vv[:, 0:32], T.i32[:], rk[0], T.coln[:, 0:1], A.is_equal, A.mult))
     need("v", k1)
     k = done("v", V.tensor_scalar(T.vv[:, 32:64], T.i32[:], rk[1], T.coln[:, 1:2], A.is_equal, A.mult))
-    need("v", k_b)
     done("v", V.tensor_scalar(T.mk[:, 0:32], T.ai[:], p4, OUT, A.not_equal, A.mult))
     need("v", k)
     for a in range(2):
@@ -220,71 +224,64 @@ def rank_program(g, core, T, topo):
     done("v", V.tensor_scalar(T.mk[:, 32:64], T.bi[:], p16, OUT, A.not_equal, A.mult))
     need("v", k)
     k = done("v", V.tensor_reduce(T.q4[0:64, 0:1], T.vt[0:64, :], X, A.add))
+    done("v", V.tensor_scalar(T.r16[:], T.bi[:], 0.0, None, A.is_gt))
     need("v", k)
     for a in range(4):
         k = done("v", V.tensor_scalar(T.xx[32 * a:32 * a + 32, :], T.mk[0:32, :], T.q4[0:32, 0:1], T.q4[32:64, 0:1], A.add, A.add))
+    need("v", k_4)
+    done("v", V.tensor_scalar(T.r4[:], T.k4[:, 0:32], 0.0, None, A.is_gt))
     need("v", k)
     k = done("v", V.transpose(T.xt[:], T.xx[:]))
+    done("v", V.tensor_scalar(T.y48[:, 0:4], T.k4[:, 0:4], pq4, 1.0 / HOLD, A.is_le, A.max))
     need("v", k)
-    k4 = done("v", V.tensor_tensor_scan(T.sg4[:], T.r4[:], T.xt[:, 0:32], 0.0, A.mult, A.max))
     k8 = done("v", V.tensor_tensor_scan(T.sg16[:], T.r16[:], T.xt[:, 32:64], 0.0, A.mult, A.max))
-    need("v", k4)
-    k_o = done("v", V.tensor_scalar(T.ofo[:], T.sg4[:, 3:32:4], 4.0, p4, A.mult, A.add))
+    k4 = done("v", V.tensor_tensor_scan(T.sg4[:], T.r4[:], T.xt[:, 0:32], 0.0, A.mult, A.max))
     need("v", k8)
     k_lp = done("v", V.tensor_scalar(T.lp[:, 0:2], T.sg16[:, 15:32:16], 8.0, float(rank), A.mult, A.add))
+    need("v", k4)
+    k_o = done("v", V.tensor_scalar(T.ofo[:], T.sg4[:, 3:32:4], 4.0, p4, A.mult, A.add))
     h0 = 4 * (own0 - q0)
     need("s", k_o, d_h)
     a_h = done("s", S.activation(T.hb[:, h0 + 64:h0 + 128], T.grb[:, 0:1024].indirect(T.ofo[:, 4:8]), AF.Copy))
+    k_y = done("v", V.tensor_scalar(T.y48[:, 8:16], T.k8[:, 0:8], pq8, 1.0 / HOLD, A.is_le, A.max))
     need("v", k_o, d_h)
     k = done("v", V.tensor_copy(T.hb[:, h0:h0 + 64], T.grb[:, 0:1024].indirect(T.ofo[:, 0:4])))
+    done("v", V.tensor_reduce(x4, T.y48[:, 0:4], X, A.mult))
     need("v", k, a_h)
     k_q = done("v", V.quantize_mx(T.qb[:, q0:q0 + 128], T.qs[:, q0:q0 + 128], T.hb[:]))
     a_e = done("s", S.activation(T.erb[:], T.grb[:], AF.Copy))
-    mine = T.ll[:, 2 * rank:2 * rank + 2]
+    mine = T.ll[:, 2 * at_l:2 * at_l + 2]
     need("y", k_lp)
     d_l = done("dl", Y.dma_start(mine, T.lp[:, 0:2]), 16)
 
     b8 = dt.uint8
-    LL, C1, S1 = ("l1", n1 + len(others) * n2), ("c1", n1), ("s1", n1)
+    L1, L2, C1, S1 = ("l1", len(peers) * n2), ("l2", n1 + (len(others) - len(peers)) * n2), ("c1", n1), ("s1", n1)
     C2, S2 = ("c2", 3 * n2), ("s2", 3 * n2)
+
+    def lists(cores, mask, sem):
+        return RemoteDMATransfer(dst_ids=ids(cores), dma_engine_mask=mask, remote_sem=T.sem[sem], srcs=[T.lp[:, 0:2]], dsts=[mine for c in cores])
+
     need("p", k_lp)
-    g.remote_dma_fused([
-        RemoteDMATransfer(dst_ids=ids(others), dma_engine_mask=m2, remote_sem=T.sem.l1, srcs=[T.lp[:, 0:2]], dsts=[mine for c in others]),
-        RemoteDMATransfer(dst_ids=ids([partner]), dma_engine_mask=m1, remote_sem=T.sem.l1, srcs=[T.lp[:, 0:2]], dsts=[mine]),
-    ], local_sem=T.sem.sent)
+    g.remote_dma_fused([lists(peers, m2, "l1")], local_sem=T.sem.sent)
     need("p", k_q)
-    rid, pid = topo.addr(partner, core)
-    g.remote_dma(out_ap=T.qb[:, far_c:far_c + 32].bitcast(b8), in_ap=T.qb[:, own0:own0 + 32].bitcast(b8), remote_sem=T.sem.c1,
-                 local_sem=T.sem.sent, pid=pid, routing_id=rid, dma_engine_mask=m1)
     hs = 0 if first else 32
     g.remote_dma_fused([RemoteDMATransfer(dst_ids=ids(helpers + [partner]), dma_engine_mask=m1, remote_sem=T.sem.s1,
                                           srcs=[T.qs[:, own0:own0 + 32]],
                                           dsts=[T.qs[:, hs:hs + 32] for h in helpers] + [T.qs[:, far_c:far_c + 32]])], local_sem=T.sem.sent)
-    cnt["sent"] += 3 * n1 + n2
+    rid, pid = topo.addr(partner, core)
+    g.remote_dma(out_ap=T.qb[:, far_c:far_c + 32].bitcast(b8), in_ap=T.qb[:, own0:own0 + 32].bitcast(b8), remote_sem=T.sem.c1,
+                 local_sem=T.sem.sent, pid=pid, routing_id=rid, dma_engine_mask=m1)
+    g.remote_dma_fused([lists([c for c in others if c not in peers], m2, "l2"), lists([partner], m1, "l2")], local_sem=T.sem.sent)
+    cnt["sent"] += 3 * n1 + 2 * n2
     need("p", C1)
     hop2(lambda i: T.cb[:, 64 * i:64 * i + 64].bitcast(b8), T.qb[:, pair0:pair0 + 64].bitcast(b8), "c2", "left")
     cnt["left"] += n2
 
-    k_e = tile_e(3)
-    f4, f8, e4, e8, x4, x8, pl, ps = [T.pf[:, 6 + i:7 + i] for i in range(8)]
-    need("v", k_kk)
-    done("v", V.tensor_scalar(f4, pq4, 1.0, None, A.add))
-    k = done("v", V.tensor_scalar(f8, pq8, 1.0, None, A.add))
-    done("v", V.tensor_scalar(e4, pq4, 3.0, 2.0, A.is_equal, A.mult))
-    c = done("v", V.tensor_scalar(e8, pq8, 7.0, 2.0, A.is_equal, A.mult))
-    done("v", V.tensor_scalar(pl, ph, float(BB), p1, A.mult, A.add))
-    done("v", V.tensor_scalar(ps, pq8, -0.125, None, A.mult))
-    need("v", k)
-    done("v", V.tensor_scalar(T.ce[:, 0:32], T.k8[:], f8, HOLD, A.is_equal, A.mult))
-    done("v", V.tensor_scalar(T.ce[:, 32:64], T.k4[:], f4, HOLD, A.is_equal, A.mult))
-    done("v", V.tensor_scalar(T.cg[:, 0:32], T.k8[:], f8, None, A.is_gt))
-    k = done("v", V.tensor_scalar(T.cg[:, 32:64], T.k4[:], f4, None, A.is_gt))
-    need("v", c)
-    done("v", V.tensor_scalar(x4, e4, 2.0 / HOLD, None, A.max))
-    done("v", V.tensor_scalar(x8, e8, 2.0 / HOLD, None, A.max))
-    need("v", k)
-    done("v", V.tensor_tensor(T.ch8[:, 0:32], T.ce[:, 0:32], T.cg[:, 0:32], A.max))
-    a_ch = done("v", V.tensor_tensor(T.ch4[:, 0:32], T.ce[:, 32:64], T.cg[:, 32:64], A.max))
+    for b in range(1, 4):
+        k_e = tile_e(b)
+    done("v", V.tensor_reduce(x8, T.y48[:, 8:16], X, A.mult))
+    done("v", V.tensor_scalar(T.ch8[:], T.k8[:], pq8, HOLD, A.is_gt, A.mult))
+    k_ch = done("v", V.tensor_scalar(T.ch4[:], T.k4[:], pq4, HOLD, A.is_gt, A.mult))
 
     def decode(ps, n, codes, scales):
         return [done("t", P.matmul_mx(ps[:, 512 * b:512 * b + n], T.eq[:, 128 * b:128 * b + 128], T.es[:, 128 * b:128 * b + 128],
@@ -298,37 +295,25 @@ def rank_program(g, core, T, topo):
 
     need("t", k_e, a_f[1], k_q)
     td = decode(T.pa, 128, T.qb[:, q0:q0 + 128], T.qs[:, q0:q0 + 128])
-    vo = [empty("s" if b % 2 else "v", td[b], T.vo[:, b:128:4], T.pa[:, 512 * b + own0 - q0:512 * b + own0 - q0 + 32]) for b in range(4)]
     need("s", k1)
     for h in range(2):
         a_rk = done("s", S.activation(T.rkf[:, h:h + 1], rk[h], AF.Copy))
-    a_r = ones(1)
-    need("v", a_e, *vo)
-    k = done("v", V.tensor_tensor(T.te[:], T.erb[:, 0:1024].indirect(T.ofo[:, 0:8]), T.vo[:], A.subtract))
+    vo = [empty("s" if b % 2 else "v", td[b], T.vo[:, b:128:4], T.pa[:, 512 * b + own0 - q0:512 * b + own0 - q0 + 32]) for b in range(4)]
+    a_r = resets(5, 8)
     need("v", a_rk)
     done("v", V.tensor_scalar(T.wv[:, 0:32], T.i32[:], T.rkf[:, 0:1], T.sth[:, 0:1], A.is_equal, A.mult))
     w = done("v", V.tensor_scalar(T.wv[:, 32:64], T.i32[:], T.rkf[:, 1:2], T.sth[:, 1:2], A.is_equal, A.mult))
+    need("v", a_e, *vo)
+    k = done("v", V.tensor_tensor(T.te[:], T.erb[:, 0:1024].indirect(T.ofo[:, 0:8]), T.vo[:], A.subtract))
+    need("v", w)
+    for a in range(2):
+        w = done("v", V.transpose(T.wt2[0:64, 64 * a:64 * a + 64], T.wv[64 * a:64 * a + 64, :]))
     need("v", k)
     k_er = done("v", V.tensor_copy(T.erb[:, 0:1024].indirect(T.ofo[:, 0:8]), T.te[:]))
     need("y", k_er, ("left", n2))
     d_er = done("der", Y.dma_start(T.er[:], T.erb[:]), 16)
     need("v", w)
-    for a in range(2):
-        w = done("v", V.transpose(T.wt2[0:64, 64 * a:64 * a + 64], T.wv[64 * a:64 * a + 64, :]))
-    need("v", a_r)
-    k_r = done("v", V.memset(T.rst[:, 0:2048:8], 0.0))
-    need("v", w)
     w = done("v", V.tensor_reduce(T.wq[0:64, 0:1], T.wt2[0:64, :], X, A.add))
-    need("v", w)
-    w = done("v", V.tensor_scalar(T.wx[0:32, 0:1], T.wq[0:32, 0:1], T.wq[32:64, 0:1], TINY, A.add, A.subtract))
-    need("v", w)
-    w = done("v", V.transpose(T.wy[0:32, :], T.wx[0:32, :]))
-    need("y", w)
-    d_sc = done("dsc", Y.dma_start(T.sc[:], T.wy[0:1, :]), 16)
-    for n in (32, 64, 128):
-        need("s", a_ch)
-        done("s", S.activation(T.ch8[:, n:2 * n], T.ch8[:, 0:n], AF.Copy))
-        a_ch = done("s", S.activation(T.ch4[:, n:2 * n], T.ch4[:, 0:n], AF.Copy))
 
     need("t", C1, S1, *vo)
     td = decode(T.pa, 128, T.qb[:, dec0:dec0 + 128], T.qs[:, dec0:dec0 + 128])
@@ -340,74 +325,69 @@ def rank_program(g, core, T, topo):
         else:
             a_p = empty("s", td[b], T.vb[:, 512 * h + i:512 * h + 128:2], T.pa[:, c0:c0 + 64])
 
-    need("v", LL, d_l, a_en, d_m, a_ch, k_r)
-    k = done("v", V.tensor_copy(T.m8[:, 0:2048].indirect(T.ll[:, 0:16]), T.ent[:]))
-    n = done("v", V.tensor_copy(T.lf[0:32, 0:16], T.ll[0:32, 0:16]))
-    need("v", k)
+    def to_map(a):
+        return done("v", V.tensor_copy(T.m8[:, 0:2048].indirect(T.ll[:, 8 * a:8 * a + 8]), T.ent[:, 128 * a:128 * a + 128]))
+
+    need("v", L1, d_l, a_en, d_m)
+    k = to_map(at_l // 4)
+    need("v", w)
+    w = done("v", V.tensor_scalar(T.wx[0:32, 0:1], T.wq[0:32, 0:1], T.wq[32:64, 0:1], TINY, A.add, A.subtract))
+    need("v", k, w)
+    w = done("v", V.transpose(T.wy[0:32, :], T.wx[0:32, :]))
+    need("y", w)
+    d_sc = done("dsc", Y.dma_start(T.sc[:], T.wy[0:1, :]), 16)
+    need("v", L2)
+    k = to_map(1 - at_l // 4)
+    n = done("v", V.tensor_scalar(T.lf[0:32, 0:16], T.ll[0:32, 0:16], -3.5, 0.125, A.add, A.mult))
+    need("v", k, a_r)
     k = done("v", V.tensor_tensor_scan(T.mp[:, 1:2049], T.rst[:], T.m8[:], 0.0, A.mult, A.max))
     need("v", n)
     n = done("v", V.transpose(T.nt[0:32, :], T.lf[0:32, :]))
     need("v", k)
     k = done("v", V.tensor_copy(T.pr[:, 0:224], T.mp[:, 0:2048].indirect(T.ll[:, 2:16])))
     need("v", n)
-    k_nb = done("v", V.tensor_scalar(T.nu[0:32, :], T.nt[0:32, :], 0.125, T.pf[0:32, 13:14], A.mult, A.add))
+    k_nb = done("v", V.tensor_scalar(T.nu[0:32, :], T.nt[0:32, :], ROUND, ROUND, A.add, A.subtract))
     need("v", k)
     k = done("v", V.tensor_tensor_scan(T.hp[:, 0:224], T.ch8[:, 0:224], T.pr[:, 0:224], 0.0, A.mult, A.add))
+    k_hl = done("v", V.tensor_tensor_scan(T.hl[:], T.ch4[:], T.mp[:, 8:2049:8], 0.0, A.mult, A.add))
     need("v", k)
     k_op = done("v", V.tensor_scalar(T.offp[:, 0:28], T.hp[:, 7:224:8], x8, p1, A.mult, A.add))
+    need("v", k_hl)
+    k_ol = done("v", V.tensor_scalar(T.offl[:], T.hl[:, 3:256:4], x4, pl, A.mult, A.add))
     need("y", k_nb)
-    d_nb = done("dnb", Y.dma_start(T.nb[:], T.nu[0:16, 0:16]), 16)
+    for a in range(2):
+        d_nb = done("dnb", Y.dma_start(T.nb[order[4 * a]:8:2, :], T.nu[8 * a:8 * a + 8, 0:16]), 16)
 
     need("t", C2, S2)
     td = decode(T.pb, 192, T.cb[:], T.cs[:])
     got = [[], []]
-
-    def landed(b, part):
+    for b in range(4):
         h, i, q, n = b // 2, b % 2, "s" if b % 2 else "v", 0 if me == 0 else 32
-        if part == 0 and n:
+        if n:
             got[h].append(empty(q, td[b], T.tv[:, BB * h + 2 + i:BB * h + 66:2], T.pb[:, 512 * b:512 * b + 32]))
-        if part == 1:
-            got[h].append(empty(q, td[b], T.vb[:, 512 * h + 128 + 2 * n + i:512 * h + 512:2], T.pb[:, 512 * b + n:512 * b + 192]))
-
-    for b in (0, 1, 3):
-        landed(b, 0)
-        landed(b, 1)
+        got[h].append(empty(q, td[b], T.vb[:, 512 * h + 128 + 2 * n + i:512 * h + 512:2], T.pb[:, 512 * b + n:512 * b + 192]))
 
     last = [None, None]
-
-    def add(h, s):
-        m = s // 2
+    for s in range(1, 8):
+        m, o = s // 2, 4 * order.index(s) - 4
         at = (s % 2) if m == me else 2 + 2 * slot(m, me) + s % 2
-        need("v", k_op, a_p, *got[h])
-        if last[h]:
-            need("v", last[h])
-        last[h] = done("v", V.tensor_tensor(T.tv[:, BB * h + 2 + 64 * s:BB * h + 66 + 64 * s],
-                                            T.tv[:, BB * h:BB * h + 2 + 64 * s].indirect(T.offp[:, 4 * s - 4:4 * s]),
-                                            T.vb[:, 512 * h + 64 * at:512 * h + 64 * at + 64], A.add))
-
-    for s in range(1, 10):
-        if s < 8:
-            add(0, s)
-        if s < 3:
-            landed(2, s - 1)
-        else:
-            add(1, s - 2)
-        if s == 7:
-            k_hl = done("v", V.tensor_tensor_scan(T.hl[:], T.ch4[:], T.mp[:, 8:2049:8], 0.0, A.mult, A.add))
-        if s == 8:
-            need("v", k_hl)
-            k_ol = done("v", V.tensor_scalar(T.offl[:], T.hl[:, 3:256:4], x4, pl, A.mult, A.add))
+        for h in range(2):
+            need("v", k_op, a_p, *got[h])
+            if last[h]:
+                need("v", last[h])
+            last[h] = done("v", V.tensor_tensor(T.tv[:, BB * h + 2 + 64 * s:BB * h + 66 + 64 * s],
+                                                T.tv[:, BB * h:BB * h + 2 + 64 * s].indirect(T.offp[:, o:o + 4]),
+                                                T.vb[:, 512 * h + 64 * at:512 * h + 64 * at + 64], A.add))
 
     need("v", k_ol, *last)
     need("s", k_ol, *last)
-    win, parts = T.tv[:, 0:BB + 514], []
-    for i in range(2):
-        parts.append((256 * i, done("v", V.tensor_copy(T.acb[:, 256 * i:256 * i + 256], win.indirect(T.offl[:, 16 * i:16 * i + 16])))))
-        parts.append((512 + 256 * i, done("s", S.activation(T.acb[:, 512 + 256 * i:768 + 256 * i], win.indirect(T.offl[:, 32 + 16 * i:48 + 16 * i]), AF.Copy))))
-    for c, tok in parts:
-        q = "s" if tok == parts[-1][1] else "y"
-        need(q, tok)
-        d_ac = done("dac", Q[q].dma_start(T.acc[:, c:c + 256], T.acb[:, c:c + 256]), 16)
+    win = T.tv[:, 0:BB + 514]
+    for a, b in zip(PIECES, PIECES[1:]):
+        m = (a + b) // 2
+        k = done("v", V.tensor_copy(T.acb[:, a:m], win.indirect(T.offl[:, a // 16:m // 16])))
+        n = done("s", S.activation(T.acb[:, m:b], win.indirect(T.offl[:, m // 16:b // 16]), AF.Copy))
+        need("y", k, n)
+        d_ac = done("dac", Y.dma_start(T.acc[:, a:b], T.acb[:, a:b]), 16)
 
-    need("p", d_u, d_1, d_2, d_h, d_m, d_l, d_er, d_nb, d_ac, d_sc, LL, C2, S2)
+    need("p", d_u, d_1, d_2, d_h, d_m, d_l, d_er, d_nb, d_ac, d_sc, L1, L2, C2, S2)
     need("p", *[(x, cnt[x]) for x in ("v", "s", "t", "p", "sent", "left")])

@@ -6,7 +6,6 @@ TINY = 2.0 ** -120
 PRED = 1.0 - 2.0 ** -24
 HOLD = 2.0 ** 14
 ROUND = 1.5 * 2.0 ** 23
-OUT = -4096.0
 BB = 520
 PIECES = (0, 256, 640, 1024)
 
@@ -20,28 +19,23 @@ SCRATCH = {
     "eq": ("sbuf", [128, 512], C8), "es": ("sbuf", [128, 512], S8),
     "qb": ("sbuf", [128, 160], C8), "qs": ("sbuf", [128, 160], S8),
     "cb": ("sbuf", [128, 192], C8), "cs": ("sbuf", [128, 192], S8),
-    "lp": ("sbuf", [128, 16], U), "ll": ("sbuf", [128, 16], U), "ofo": ("sbuf", [128, 8], U),
-    "offp": ("sbuf", [128, 32], U), "offl": ("sbuf", [128, 64], U),
+    "lp": ("sbuf", [128, 16], U), "ll": ("sbuf", [128, 16], U), "ofo": ("sbuf", [128, 8], U), "oc": ("sbuf", [128, 8], U),
+    "offp": ("sbuf", [128, 32], U), "offl": ("sbuf", [128, 32], U),
     "ab": ("sbuf", [128, 256], F), "th": ("sbuf", [128, 256], F), "wt": ("sbuf", [128, 128], F),
-    "sth": ("sbuf", [128, 8], F),
-    "cmp": ("sbuf", [128, 512], B), "rks": ("sbuf", [128, 256], B), "rkf": ("sbuf", [128, 8], F),
-    "i32": ("sbuf", [128, 32], F), "coln": ("sbuf", [128, 2], B), "pi": ("sbuf", [128, 8], I), "pf": ("sbuf", [128, 16], F),
-    "ai": ("sbuf", [128, 32], F), "bi": ("sbuf", [128, 32], F), "k4": ("sbuf", [128, 256], B), "k8": ("sbuf", [128, 256], B),
-    "mk": ("sbuf", [128, 64], F), "r4": ("sbuf", [128, 32], F), "r16": ("sbuf", [128, 32], F),
-    "y48": ("sbuf", [128, 16], F), "ch4": ("sbuf", [128, 256], B), "ch8": ("sbuf", [128, 256], B),
-    "vv": ("sbuf", [128, 64], F), "vt": ("sbuf", [128, 128], F), "q4": ("sbuf", [128, 8], F),
-    "xx": ("sbuf", [128, 64], F), "xt": ("sbuf", [128, 64], F), "sg4": ("sbuf", [128, 32], F), "sg16": ("sbuf", [128, 32], F),
-    "wv": ("sbuf", [128, 64], F), "wt2": ("sbuf", [128, 128], F), "wq": ("sbuf", [128, 8], F), "wx": ("sbuf", [128, 32], F),
-    "wy": ("sbuf", [128, 32], F), "zz": ("sbuf", [128, 16], F), "zt": ("sbuf", [128, 512], B),
+    "sth": ("sbuf", [128, 8], F), "scb": ("sbuf", [128, 32], F),
+    "cmp": ("sbuf", [128, 512], B), "rks": ("sbuf", [128, 256], B),
+    "i32": ("sbuf", [128, 32], F), "coln": ("sbuf", [128, 2], B), "pi": ("sbuf", [128, 40], I), "pf": ("sbuf", [128, 16], F),
+    "bi": ("sbuf", [128, 64], F), "k8": ("sbuf", [128, 256], B), "y8": ("sbuf", [128, 8], F), "ch8": ("sbuf", [128, 256], B),
+    "vv": ("sbuf", [128, 128], B), "vt": ("sbuf", [128, 256], B), "sq": ("sbuf", [128, 128], B),
+    "zt": ("sbuf", [128, 512], B),
     "lf": ("sbuf", [128, 32], F), "nt": ("sbuf", [128, 32], F), "nu": ("sbuf", [128, 32], F),
     "ent": ("sbuf", [128, 256], B), "m8": ("sbuf", [128, 2048], B), "rst": ("sbuf", [128, 2048], B), "mp": ("sbuf", [128, 2064], B),
     "pr": ("sbuf", [128, 256], B), "hp": ("sbuf", [128, 256], B), "hl": ("sbuf", [128, 256], B),
     "tv": ("sbuf", [128, 1040], F),
-    "acb": ("sbuf", [128, 1024], F), "erb": ("sbuf", [128, 1024], F), "vb": ("sbuf", [128, 1024], F),
-    "vo": ("sbuf", [128, 128], F), "te": ("sbuf", [128, 128], F),
+    "acb": ("sbuf", [128, 1024], F), "erb": ("sbuf", [128, 1024], F), "te": ("sbuf", [128, 128], F),
     "pa": ("psum", [128, 2048], F), "pb": ("psum", [128, 2048], F),
 }
-SEMAPHORES = ["v", "s", "t", "p", "dg1", "dg2", "du", "dl", "dh", "dm", "dsc", "dnb", "der", "dac", "l1", "l2", "c1", "s1", "c2", "s2",
+SEMAPHORES = ["v", "s", "t", "p", "dg1", "dg2", "du", "dl", "dh", "dm", "dsc", "dnb", "der", "dac", "l1", "l2", "c1", "s1", "a2", "b2",
               "sent", "left"]
 
 
@@ -53,7 +47,8 @@ def rank_program(g, core, T, topo):
     others = [c for c in T.cores if c not in chip]
     peers = [c for c in others if topo.die(c) == topo.die(core)]
     helpers = [h for h in chip if h not in ranks and all(topo.may_write(h, c) for c in others)]
-    if core not in ranks and core not in helpers:
+    aides = {c: min(a for a in chip if a not in ranks + helpers and topo.die(a) == topo.die(c)) for c in ranks}
+    if core not in ranks + helpers + list(aides.values()):
         return
 
     def pair(c):
@@ -61,25 +56,33 @@ def rank_program(g, core, T, topo):
 
     me = pair(core)
 
-    def slot(src, dst):
-        return src - (1 if src > dst else 0)
+    peers.sort(key=lambda c: (topo.same_plane(core, c), topo.mates(core, c)))
 
     def ids(cores):
         a = [topo.addr(c, core) for c in cores]
         return [DstId(rid=r_, pnc=p_) for r_, p_ in a]
 
-    m2 = topo.mask(core, others[0])
-    for c in others:
-        m2 &= topo.mask(core, c)
+    m2 = topo.mask(core, peers[2])
     n2 = bin(m2).count("1")
+    b8 = dt.uint8
 
-    def hop2(dst, src, sem, local):
-        g.remote_dma_fused([RemoteDMATransfer(dst_ids=ids(peers), dma_engine_mask=m2, remote_sem=T.sem[sem], srcs=[src],
-                                              dsts=[dst(slot(me, pair(c))) for c in peers])], local_sem=T.sem[local])
+    def hop2(dst, src, local, sem, slots):
+        g.remote_dma_fused([RemoteDMATransfer(dst_ids=ids([peers[i] for i in slots]), dma_engine_mask=m2, remote_sem=T.sem[sem],
+                                              srcs=[src], dsts=[dst(i) for i in slots])], local_sem=T.sem[local])
 
     if core in helpers:
         g.wait_ge(T.sem.s1, sum(bin(topo.mask(c, core) & ~m2).count("1") for c in ranks))
-        hop2(lambda i: T.cs[:, 64 * i:64 * i + 64], T.qs[:, 0:64], "s2", "sent")
+        for sem, slots in (("a2", (0, 1)), ("b2", (2,))):
+            hop2(lambda i: T.cs[:, 64 * i:64 * i + 64], T.qs[:, 0:64], "sent", sem, slots)
+        g.wait_ge(T.sem.sent, 2 * n2)
+        return
+    if core not in ranks:
+        src = [c for c in ranks if aides[c] == core][0]
+        at = 128 + 32 * ranks.index(src)
+        far = [c for c in others if topo.same_plane(core, c)]
+        g.wait_ge(T.sem.c1, bin(topo.mask(src, core) & ~m2).count("1"))
+        g.remote_dma_fused([RemoteDMATransfer(dst_ids=ids(far), dma_engine_mask=m2, remote_sem=T.sem.b2, srcs=[T.qb[:, 0:32].bitcast(b8)],
+                                              dsts=[T.cb[:, at:at + 32].bitcast(b8) for c in far])], local_sem=T.sem.sent)
         g.wait_ge(T.sem.sent, n2)
         return
 
@@ -120,37 +123,32 @@ def rank_program(g, core, T, topo):
     def iota(buf, pattern, base, cm):
         return done("p", g.iota(buf, pattern, base, cm, allow_small_or_imprecise_dtypes=True))
 
-    k = done("v", V.memset(T.eb[:], 0.0))
-    done("v", V.memset(T.zz[:], 0.0))
-    k_wt = done("v", V.memset(T.wt[:], PRED))
-    need("v", k)
-    e3 = T.eb[:, 3:515:4]
-    k_eb = done("v", V.memset(e3, 1.0))
-    k_p = done("p", g.iota(T.pi[:, 0:1], [[1, 1]], 0, 1))
+    def tile_e(b):
+        need("v", k_eb)
+        return done("v", V.quantize_mx(T.eq[:, 128 * b:128 * b + 128], T.es[:, 128 * b:128 * b + 128], T.eb[:, 3 - b:515 - b]))
+
+    done("v", V.memset(T.wt[:], PRED))
+    k_eb = done("v", V.memset(T.eb[:], 0.0))
+    k_p = done("p", g.iota(T.pi[:, 0:16], [[0, 16]], 0, 1))
+    need("v", k_p)
+    k_4 = done("v", V.tensor_scalar(T.pi[:, 16:32], T.pi[:, 0:16], 3, None, A.bitwise_and))
     k_i = iota(T.i32[:], [[1, 32]], 0, 0)
     need("p", k_eb)
-    k_eb = done("p", g.affine_select(e3, e3, [[-1, 128]], A.is_equal, 0.0, 0, 1))
+    k_eb = done("p", g.affine_select(T.eb[:, 3:515:4], T.wt[:], [[-1, 128]], A.is_equal, 0.0, 0, 1))
+    need("p", k_eb)
     k_wt = done("p", g.affine_select(T.wt[:], T.wt[:], [[-1, 128]], A.is_gt, 1.0, 0, 1))
     k_8 = iota(T.k8[:], [[0, 32], [1, 8]], 0, 0)
-    iota(T.ai[:], [[0, 2], [1, 4], [0, 4]], 0, 0)
-    k_b = iota(T.bi[:], [[0, 2], [1, 16]], 0, 0)
-    k_c = iota(T.coln[:], [[128, 2]], 0, 1)
-    k_4 = iota(T.k4[:], [[0, 64], [1, 4]], 0, 0)
-    need("v", k_p)
-    done("v", V.tensor_scalar(T.pi[:, 1:2], T.pi[:, 0:1], 3, None, A.bitwise_and))
-    done("v", V.tensor_scalar(T.pi[:, 2:3], T.pi[:, 0:1], 2, 3, A.logical_shift_right, A.bitwise_and))
-    done("v", V.tensor_scalar(T.pi[:, 3:4], T.pi[:, 0:1], 15, None, A.bitwise_and))
-    done("v", V.tensor_scalar(T.pi[:, 4:5], T.pi[:, 0:1], 1, None, A.bitwise_and))
-    done("v", V.tensor_scalar(T.pi[:, 5:6], T.pi[:, 0:1], 1, 7, A.logical_shift_right, A.bitwise_and))
-    k = done("v", V.tensor_scalar(T.pi[:, 6:7], T.pi[:, 0:1], 1, 1, A.logical_shift_right, A.bitwise_and))
+    iota(T.bi[:], [[16, 2], [0, 2], [1, 16]], 0, 0)
+    k_c = iota(T.coln[:], [[1024, 2]], 0, 8)
+    done("v", V.tensor_scalar(T.pi[:, 32:33], T.pi[:, 0:1], 1, None, A.bitwise_and))
+    k = done("v", V.tensor_scalar(T.pi[:, 33:34], T.pi[:, 0:1], 1, 7, A.logical_shift_right, A.bitwise_and))
+    need("v", k_4)
+    k_uo = done("v", V.tensor_copy(T.uo[:], T.pi[:, 16:32]))
     k_zt = done("v", V.memset(T.zt[:], 0.0))
     need("v", k)
-    k = done("v", V.tensor_copy(T.pf[:, 0:6], T.pi[:, 1:7]))
-    p4, pq4, p16, p1, pq8, ph = [T.pf[:, i:i + 1] for i in range(6)]
-    x4, x8, pl = [T.pf[:, 6 + i:7 + i] for i in range(3)]
-    need("v", k)
-    k_uo = done("v", V.tensor_scalar(T.uo[:], T.zz[:], p4, None, A.add))
-    done("v", V.tensor_scalar(pl, ph, float(BB), p1, A.mult, A.add))
+    done("v", V.tensor_copy(T.pf[:, 0:2], T.pi[:, 32:34]))
+    p1, pq8, x8 = [T.pf[:, i:i + 1] for i in range(3)]
+    tile_e(0)
     need("y", k_zt)
     d_h = done("dh", Y.dma_start(T.hb[:], T.zt[:]), 16)
     for a in range(4):
@@ -161,14 +159,10 @@ def rank_program(g, core, T, topo):
 
     need("s", d_u, k_uo)
     a_u = done("s", S.activation(T.urep[:, 256:512], T.ub[:, 0:4].indirect(T.uo[:, 0:16]), AF.Copy))
-    for z in (T.tv[:, 0:2], T.tv[:, 514:BB + 2], T.mp[:, 0:1], T.lf[:], T.wx[:]):
+    for z in (T.tv[:, 0:2], T.tv[:, BB:BB + 2], T.mp[:, 0:1], T.lf[:]):
         done("s", S.activation(z, T.i32[:, 0:z.shape[1]], AF.Copy, scale=0.0))
     need("v", d_u, k_uo)
     k_u = done("v", V.tensor_copy(T.urep[:, 0:256], T.ub[:, 0:4].indirect(T.uo[:, 0:16])))
-
-    def tile_e(b):
-        need("v", k_eb)
-        return done("v", V.quantize_mx(T.eq[:, 128 * b:128 * b + 128], T.es[:, 128 * b:128 * b + 128], T.eb[:, 3 - b:515 - b]))
 
     a_c, a_f = [], []
     for h in range(2):
@@ -186,7 +180,7 @@ def rank_program(g, core, T, topo):
         need("s", t_f)
         a_f.append(done("s", S.activation(T.ab[:, j:j + 128], T.pa[:, 1024 * h + 512:1024 * h + 640], AF.Abs, bias=TINY)))
         if h == 0:
-            tile_e(0)
+            tile_e(1)
 
     s0, s1 = T.sth[:, 0:1], T.sth[:, 1:2]
     need("s", k_wt, a_c[1])
@@ -208,135 +202,115 @@ def rank_program(g, core, T, topo):
     rk = [T.rks[:, 127:128], T.rks[:, 255:256]]
 
     def resets(a, b):
-        need("s", k_8)
         return [done("s", S.activation(T.rst[:, 256 * i:256 * i + 256], T.k8[:], AF.Sign)) for i in range(a, b)][-1]
 
+    need("s", k_8)
     resets(0, 5)
 
-    need("v", k_c, k0)
-    done("v", V.tensor_scalar(T.vv[:, 0:32], T.i32[:], rk[0], T.coln[:, 0:1], A.is_equal, A.mult))
-    need("v", k1)
-    k = done("v", V.tensor_scalar(T.vv[:, 32:64], T.i32[:], rk[1], T.coln[:, 1:2], A.is_equal, A.mult))
-    done("v", V.tensor_scalar(T.mk[:, 0:32], T.ai[:], p4, OUT, A.not_equal, A.mult))
+    for h in range(2):
+        need("v", k_c, (k0, k1)[h])
+        for i in range(2):
+            k = done("v", V.tensor_scalar(T.vv[:, 64 * i + 32 * h:64 * i + 32 * h + 32], T.bi[:, 32 * i:32 * i + 32], rk[h],
+                                          T.coln[:, h:h + 1], A.is_equal, A.mult))
+    tile_e(2)
     need("v", k)
     for a in range(2):
-        k = done("v", V.transpose(T.vt[0:64, 64 * a:64 * a + 64], T.vv[64 * a:64 * a + 64, :]))
-    done("v", V.tensor_scalar(T.mk[:, 32:64], T.bi[:], p16, OUT, A.not_equal, A.mult))
+        k = done("v", V.transpose(T.vt[0:64, 128 * a:128 * a + 128], T.vv[64 * a:64 * a + 64, :]))
+    k_e = tile_e(3)
     need("v", k)
-    k = done("v", V.tensor_reduce(T.q4[0:64, 0:1], T.vt[0:64, :], X, A.add))
-    done("v", V.tensor_scalar(T.r16[:], T.bi[:], 0.0, None, A.is_gt))
+    for i in range(2):
+        k = done("v", V.tensor_tensor_scan(T.sq[0:64, 64 * i:64 * i + 64], T.vt[0:64, 64 * i:64 * i + 64],
+                                           T.vt[0:64, 128 + 64 * i:192 + 64 * i], 0.0, A.add, A.add))
+    done("v", V.tensor_scalar(T.y8[:], T.k8[:, 0:8], pq8, 1.0 / HOLD, A.is_le, A.max))
+    done("v", V.tensor_scalar(T.ch8[:, 0:128], T.k8[:, 0:128], pq8, HOLD, A.is_gt, A.mult))
     need("v", k)
-    for a in range(4):
-        k = done("v", V.tensor_scalar(T.xx[32 * a:32 * a + 32, :], T.mk[0:32, :], T.q4[0:32, 0:1], T.q4[32:64, 0:1], A.add, A.add))
-    need("v", k_4)
-    done("v", V.tensor_scalar(T.r4[:], T.k4[:, 0:32], 0.0, None, A.is_gt))
-    need("v", k)
-    k = done("v", V.transpose(T.xt[:], T.xx[:]))
-    done("v", V.tensor_scalar(T.y48[:, 0:4], T.k4[:, 0:4], pq4, 1.0 / HOLD, A.is_le, A.max))
-    need("v", k)
-    k8 = done("v", V.tensor_tensor_scan(T.sg16[:], T.r16[:], T.xt[:, 32:64], 0.0, A.mult, A.max))
-    k4 = done("v", V.tensor_tensor_scan(T.sg4[:], T.r4[:], T.xt[:, 0:32], 0.0, A.mult, A.max))
-    need("v", k8)
-    k_lp = done("v", V.tensor_scalar(T.lp[:, 0:2], T.sg16[:, 15:32:16], 8.0, float(rank), A.mult, A.add))
-    need("v", k4)
-    k_o = done("v", V.tensor_scalar(T.ofo[:], T.sg4[:, 3:32:4], 4.0, p4, A.mult, A.add))
+    for i in range(2):
+        for a in range(4):
+            k_lp = done("v", V.tensor_scalar(T.lp[32 * a:32 * a + 32, i:i + 1], T.sq[0:32, 64 * i + 63:64 * i + 64],
+                                             T.sq[32:64, 64 * i + 63:64 * i + 64], float(rank), A.add, A.add))
+    done("v", V.tensor_scalar(T.ch8[:, 128:256], T.k8[:, 128:256], pq8, HOLD, A.is_gt, A.mult))
+    need("v", (k[0], k[1] + 1))
+    done("v", V.tensor_reduce(x8, T.y8[:], X, A.mult))
+    need("v", k_lp)
+    k_o = [done("v", V.tensor_scalar(T.ofo[:, 2 * t:2 * t + 2], T.lp[:, 0:2], 0.5, t - rank / 2, A.mult, A.add)) for t in range(4)]
     h0 = 4 * (own0 - q0)
-    need("s", k_o, d_h)
-    a_h = done("s", S.activation(T.hb[:, h0 + 64:h0 + 128], T.grb[:, 0:1024].indirect(T.ofo[:, 4:8]), AF.Copy))
-    k_y = done("v", V.tensor_scalar(T.y48[:, 8:16], T.k8[:, 0:8], pq8, 1.0 / HOLD, A.is_le, A.max))
-    need("v", k_o, d_h)
-    k = done("v", V.tensor_copy(T.hb[:, h0:h0 + 64], T.grb[:, 0:1024].indirect(T.ofo[:, 0:4])))
-    done("v", V.tensor_reduce(x4, T.y48[:, 0:4], X, A.mult))
+    k_oc = done("v", V.tensor_scalar(T.oc[:, 0:2], T.lp[:, 0:2], -float(rank), 0.125, A.add, A.mult))
+    for t in range(4):
+        q, dst, src = "ssvv"[t], T.hb[:, h0 + t:h0 + 128:4], T.grb[:, 0:1024].indirect(T.ofo[:, 2 * t:2 * t + 2])
+        need(q, k_o[t], d_h)
+        if q == "s":
+            a_h = done("s", S.activation(dst, src, AF.Copy))
+        else:
+            k = done("v", V.tensor_copy(dst, src))
     need("v", k, a_h)
     k_q = done("v", V.quantize_mx(T.qb[:, q0:q0 + 128], T.qs[:, q0:q0 + 128], T.hb[:]))
-    a_e = done("s", S.activation(T.erb[:], T.grb[:], AF.Copy))
     mine = T.ll[:, 2 * at_l:2 * at_l + 2]
     need("y", k_lp)
     d_l = done("dl", Y.dma_start(mine, T.lp[:, 0:2]), 16)
 
-    b8 = dt.uint8
     L1, L2, C1, S1 = ("l1", len(peers) * n2), ("l2", n1 + (len(others) - len(peers)) * n2), ("c1", n1), ("s1", n1)
-    C2, S2 = ("c2", 3 * n2), ("s2", 3 * n2)
+    A2, B2 = ("a2", 4 * n2), ("b2", 3 * n2)
 
     def lists(cores, mask, sem):
         return RemoteDMATransfer(dst_ids=ids(cores), dma_engine_mask=mask, remote_sem=T.sem[sem], srcs=[T.lp[:, 0:2]], dsts=[mine for c in cores])
 
+    def hop1(cores, sem, src, dsts):
+        g.remote_dma_fused([RemoteDMATransfer(dst_ids=ids(cores), dma_engine_mask=m1, remote_sem=T.sem[sem], srcs=[src], dsts=dsts)],
+                           local_sem=T.sem.sent)
+
     need("p", k_lp)
     g.remote_dma_fused([lists(peers, m2, "l1")], local_sem=T.sem.sent)
+    g.remote_dma_fused([lists([c for c in others if c not in peers], m2, "l2"), lists([partner], m1, "l2")], local_sem=T.sem.sent)
     need("p", k_q)
     hs = 0 if first else 32
-    g.remote_dma_fused([RemoteDMATransfer(dst_ids=ids(helpers + [partner]), dma_engine_mask=m1, remote_sem=T.sem.s1,
-                                          srcs=[T.qs[:, own0:own0 + 32]],
-                                          dsts=[T.qs[:, hs:hs + 32] for h in helpers] + [T.qs[:, far_c:far_c + 32]])], local_sem=T.sem.sent)
-    rid, pid = topo.addr(partner, core)
-    g.remote_dma(out_ap=T.qb[:, far_c:far_c + 32].bitcast(b8), in_ap=T.qb[:, own0:own0 + 32].bitcast(b8), remote_sem=T.sem.c1,
-                 local_sem=T.sem.sent, pid=pid, routing_id=rid, dma_engine_mask=m1)
-    g.remote_dma_fused([lists([c for c in others if c not in peers], m2, "l2"), lists([partner], m1, "l2")], local_sem=T.sem.sent)
-    cnt["sent"] += 3 * n1 + 2 * n2
+    hop1(helpers, "s1", T.qs[:, own0:own0 + 32], [T.qs[:, hs:hs + 32] for h in helpers])
+    hop1([aides[core], partner], "c1", T.qb[:, own0:own0 + 32].bitcast(b8), [T.qb[:, a:a + 32].bitcast(b8) for a in (0, far_c)])
+    hop1([partner], "s1", T.qs[:, own0:own0 + 32], [T.qs[:, far_c:far_c + 32]])
+    cnt["sent"] += 4 * n1 + 2 * n2
     need("p", C1)
-    hop2(lambda i: T.cb[:, 64 * i:64 * i + 64].bitcast(b8), T.qb[:, pair0:pair0 + 64].bitcast(b8), "c2", "left")
+    hop2(lambda i: T.cb[:, 64 * i:64 * i + 64].bitcast(b8), T.qb[:, pair0:pair0 + 64].bitcast(b8), "left", "a2", (0, 1))
     cnt["left"] += n2
 
-    for b in range(1, 4):
-        k_e = tile_e(b)
-    done("v", V.tensor_reduce(x8, T.y48[:, 8:16], X, A.mult))
-    done("v", V.tensor_scalar(T.ch8[:], T.k8[:], pq8, HOLD, A.is_gt, A.mult))
-    k_ch = done("v", V.tensor_scalar(T.ch4[:], T.k4[:], pq4, HOLD, A.is_gt, A.mult))
-
-    def decode(ps, n, codes, scales):
-        return [done("t", P.matmul_mx(ps[:, 512 * b:512 * b + n], T.eq[:, 128 * b:128 * b + 128], T.es[:, 128 * b:128 * b + 128],
-                                      codes, scales, True, True)) for b in range(4)]
-
-    def empty(q, tok, dst, src):
-        need(q, tok)
-        if q == "s":
-            return done("s", S.activation(dst, src, AF.Copy))
-        return done("v", V.tensor_copy(dst, src))
+    def decode(ps, codes, scales):
+        return {b: done("t", P.matmul_mx(ps[:, 512 * b:512 * b + 128], T.eq[:, 128 * b:128 * b + 128], T.es[:, 128 * b:128 * b + 128],
+                                         codes, scales, True, True)) for b in (0, 2, 1, 3)}
 
     need("t", k_e, a_f[1], k_q)
-    td = decode(T.pa, 128, T.qb[:, q0:q0 + 128], T.qs[:, q0:q0 + 128])
-    need("s", k1)
-    for h in range(2):
-        a_rk = done("s", S.activation(T.rkf[:, h:h + 1], rk[h], AF.Copy))
-    vo = [empty("s" if b % 2 else "v", td[b], T.vo[:, b:128:4], T.pa[:, 512 * b + own0 - q0:512 * b + own0 - q0 + 32]) for b in range(4)]
+    td = decode(T.pa, T.qb[:, q0:q0 + 128], T.qs[:, q0:q0 + 128])
+    a_e = done("s", S.activation(T.erb[:], T.grb[:], AF.Copy))
+    need("s", k_oc, a_f[1])
+    a_sc = done("s", S.activation(T.scb[:], T.ab[:, 0:256].indirect(T.oc[:, 0:2]), AF.Copy, bias=-TINY))
     a_r = resets(5, 8)
-    need("v", a_rk)
-    done("v", V.tensor_scalar(T.wv[:, 0:32], T.i32[:], T.rkf[:, 0:1], T.sth[:, 0:1], A.is_equal, A.mult))
-    w = done("v", V.tensor_scalar(T.wv[:, 32:64], T.i32[:], T.rkf[:, 1:2], T.sth[:, 1:2], A.is_equal, A.mult))
-    need("v", a_e, *vo)
-    k = done("v", V.tensor_tensor(T.te[:], T.erb[:, 0:1024].indirect(T.ofo[:, 0:8]), T.vo[:], A.subtract))
-    need("v", w)
-    for a in range(2):
-        w = done("v", V.transpose(T.wt2[0:64, 64 * a:64 * a + 64], T.wv[64 * a:64 * a + 64, :]))
-    need("v", k)
+    for b in td:
+        need("v", td[b])
+        k_te = done("v", V.tensor_tensor(T.te[:, 32 * b:32 * b + 32], T.hb[:, h0 + b:h0 + 128:4],
+                                         T.pa[:, 512 * b + own0 - q0:512 * b + own0 - q0 + 32], A.subtract))
+    need("v", k_te, a_e)
     k_er = done("v", V.tensor_copy(T.erb[:, 0:1024].indirect(T.ofo[:, 0:8]), T.te[:]))
+    need("y", a_sc)
+    d_sc = done("dsc", Y.dma_start(T.sc[:], T.scb[0:1, :]), 16)
     need("y", k_er, ("left", n2))
     d_er = done("der", Y.dma_start(T.er[:], T.erb[:]), 16)
-    need("v", w)
-    w = done("v", V.tensor_reduce(T.wq[0:64, 0:1], T.wt2[0:64, :], X, A.add))
 
-    need("t", C1, S1, *vo)
-    td = decode(T.pa, 128, T.qb[:, dec0:dec0 + 128], T.qs[:, dec0:dec0 + 128])
-    for b in range(4):
-        h, i, c0 = b // 2, b % 2, 512 * b + pair0 - dec0
-        if me == 0:
-            empty("s", td[b], T.tv[:, BB * h + 2 + i:BB * h + 66:2], T.pa[:, c0:c0 + 32])
-            a_p = empty("s", td[b], T.vb[:, 512 * h + 64 + i:512 * h + 128:2], T.pa[:, c0 + 32:c0 + 64])
-        else:
-            a_p = empty("s", td[b], T.vb[:, 512 * h + i:512 * h + 128:2], T.pa[:, c0:c0 + 64])
+    got = {}
+
+    def to_sum(q, tok, b, m, src):
+        a = BB * (b % 2) + 2 + 128 * m + b // 2
+        need(q, tok)
+        dst = T.tv[:, a:a + 127:2]
+        got.setdefault((b % 2, m), []).append(done(q, S.activation(dst, src, AF.Copy) if q == "s" else V.tensor_copy(dst, src)))
+
+    need("t", C1, S1, k_te)
+    td = decode(T.pa, T.qb[:, dec0:dec0 + 128], T.qs[:, dec0:dec0 + 128])
+    for b in td:
+        to_sum("s", td[b], b, me, T.pa[:, 512 * b + pair0 - dec0:512 * b + pair0 - dec0 + 64])
 
     def to_map(a):
         return done("v", V.tensor_copy(T.m8[:, 0:2048].indirect(T.ll[:, 8 * a:8 * a + 8]), T.ent[:, 128 * a:128 * a + 128]))
 
     need("v", L1, d_l, a_en, d_m)
     k = to_map(at_l // 4)
-    need("v", w)
-    w = done("v", V.tensor_scalar(T.wx[0:32, 0:1], T.wq[0:32, 0:1], T.wq[32:64, 0:1], TINY, A.add, A.subtract))
-    need("v", k, w)
-    w = done("v", V.transpose(T.wy[0:32, :], T.wx[0:32, :]))
-    need("y", w)
-    d_sc = done("dsc", Y.dma_start(T.sc[:], T.wy[0:1, :]), 16)
-    need("v", L2)
+    need("v", k, L2)
     k = to_map(1 - at_l // 4)
     n = done("v", V.tensor_scalar(T.lf[0:32, 0:16], T.ll[0:32, 0:16], -3.5, 0.125, A.add, A.mult))
     need("v", k, a_r)
@@ -345,49 +319,42 @@ def rank_program(g, core, T, topo):
     n = done("v", V.transpose(T.nt[0:32, :], T.lf[0:32, :]))
     need("v", k)
     k = done("v", V.tensor_copy(T.pr[:, 0:224], T.mp[:, 0:2048].indirect(T.ll[:, 2:16])))
+    k_hl = done("v", V.tensor_tensor_scan(T.hl[:], T.ch8[:], T.mp[:, 8:2049:8], 0.0, A.mult, A.add))
+    need("v", k)
+    k = done("v", V.tensor_tensor_scan(T.hp[:, 0:224], T.ch8[:, 0:224], T.pr[:, 0:224], 0.0, A.mult, A.add))
     need("v", n)
     k_nb = done("v", V.tensor_scalar(T.nu[0:32, :], T.nt[0:32, :], ROUND, ROUND, A.add, A.subtract))
     need("v", k)
-    k = done("v", V.tensor_tensor_scan(T.hp[:, 0:224], T.ch8[:, 0:224], T.pr[:, 0:224], 0.0, A.mult, A.add))
-    k_hl = done("v", V.tensor_tensor_scan(T.hl[:], T.ch4[:], T.mp[:, 8:2049:8], 0.0, A.mult, A.add))
-    need("v", k)
     k_op = done("v", V.tensor_scalar(T.offp[:, 0:28], T.hp[:, 7:224:8], x8, p1, A.mult, A.add))
-    need("v", k_hl)
-    k_ol = done("v", V.tensor_scalar(T.offl[:], T.hl[:, 3:256:4], x4, pl, A.mult, A.add))
     need("y", k_nb)
     for a in range(2):
         d_nb = done("dnb", Y.dma_start(T.nb[order[4 * a]:8:2, :], T.nu[8 * a:8 * a + 8, 0:16]), 16)
 
-    need("t", C2, S2)
-    td = decode(T.pb, 192, T.cb[:], T.cs[:])
-    got = [[], []]
-    for b in range(4):
-        h, i, q, n = b // 2, b % 2, "s" if b % 2 else "v", 0 if me == 0 else 32
-        if n:
-            got[h].append(empty(q, td[b], T.tv[:, BB * h + 2 + i:BB * h + 66:2], T.pb[:, 512 * b:512 * b + 32]))
-        got[h].append(empty(q, td[b], T.vb[:, 512 * h + 128 + 2 * n + i:512 * h + 512:2], T.pb[:, 512 * b + n:512 * b + 192]))
+    for tok, ps, c0, slots, qs in ((A2, T.pb, 0, (0, 1), "ssss"), (B2, T.pa, 64, (2,), "vsvs")):
+        need("t", tok, *got[1, me])
+        td = decode(ps, T.cb[:, c0:c0 + 128], T.cs[:, c0:c0 + 128])
+        for b in td:
+            for i in slots:
+                to_sum(qs[b], td[b], b, pair(peers[i]), ps[:, 512 * b + 64 * i - c0:512 * b + 64 * i - c0 + 64])
+    need("v", k_hl)
+    k_ol = done("v", V.tensor_scalar(T.offl[:], T.hl[:, 7:256:8], x8, p1, A.mult, A.add))
 
     last = [None, None]
-    for s in range(1, 8):
-        m, o = s // 2, 4 * order.index(s) - 4
-        at = (s % 2) if m == me else 2 + 2 * slot(m, me) + s % 2
-        for h in range(2):
-            need("v", k_op, a_p, *got[h])
-            if last[h]:
-                need("v", last[h])
-            last[h] = done("v", V.tensor_tensor(T.tv[:, BB * h + 2 + 64 * s:BB * h + 66 + 64 * s],
-                                                T.tv[:, BB * h:BB * h + 2 + 64 * s].indirect(T.offp[:, o:o + 4]),
-                                                T.vb[:, 512 * h + 64 * at:512 * h + 64 * at + 64], A.add))
+    for h, s in [(h, s) for s in range(1, 8) for h in range(2)]:
+        o, own = 4 * order.index(s) - 4, T.tv[:, BB * h + 2 + 64 * s:BB * h + 66 + 64 * s]
+        need("v", k_op, *got[h, s // 2], *got[h, 0])
+        if last[h]:
+            need("v", last[h])
+        last[h] = done("v", V.tensor_tensor(own, T.tv[:, BB * h:BB * h + 2 + 64 * s].indirect(T.offp[:, o:o + 4]), own, A.add))
 
-    need("v", k_ol, *last)
-    need("s", k_ol, *last)
-    win = T.tv[:, 0:BB + 514]
+    need("s", k_ol, last[0])
+    need("v", k_ol, last[1])
     for a, b in zip(PIECES, PIECES[1:]):
-        m = (a + b) // 2
-        k = done("v", V.tensor_copy(T.acb[:, a:m], win.indirect(T.offl[:, a // 16:m // 16])))
-        n = done("s", S.activation(T.acb[:, m:b], win.indirect(T.offl[:, m // 16:b // 16]), AF.Copy))
+        off = T.offl[:, a // 32:b // 32]
+        n = done("s", S.activation(T.acb[:, a:b:2], T.tv[:, 0:514].indirect(off), AF.Copy))
+        k = done("v", V.tensor_copy(T.acb[:, a + 1:b:2], T.tv[:, BB:BB + 514].indirect(off)))
         need("y", k, n)
         d_ac = done("dac", Y.dma_start(T.acc[:, a:b], T.acb[:, a:b]), 16)
 
-    need("p", d_u, d_1, d_2, d_h, d_m, d_l, d_er, d_nb, d_ac, d_sc, L1, L2, C2, S2)
+    need("p", d_u, d_1, d_2, d_h, d_m, d_l, d_er, d_nb, d_ac, d_sc, L1, L2, A2, B2)
     need("p", *[(x, cnt[x]) for x in ("v", "s", "t", "p", "sent", "left")])

from concourse.bass import DstId, RemoteDMATransfer
from concourse.mybir import dt, AluOpType, AxisListType, ActivationFunctionType

K = 32
TINY = 2.0 ** -120
PRED = 1.0 - 2.0 ** -24
HOLD = 2.0 ** 14
ROUND = 1.5 * 2.0 ** 23
BB = 520
PIECES = (0, 256, 640, 1024)

F, B, I, U = "float32", "bfloat16", "int32", "uint16"
C8, S8 = "float8_e4m3fn_x4", "uint8"
SCRATCH = {
    "grb": ("sbuf", [128, 1024], B), "ub": ("sbuf", [128, 16], B), "urep": ("sbuf", [128, 512], B), "hb": ("sbuf", [128, 512], B),
    "eb": ("sbuf", [128, 528], B), "uo": ("sbuf", [128, 16], U),
    "gq": ("sbuf", [128, 256], C8), "gs": ("sbuf", [128, 256], S8),
    "uq": ("sbuf", [128, 128], C8), "us": ("sbuf", [128, 128], S8),
    "eq": ("sbuf", [128, 512], C8), "es": ("sbuf", [128, 512], S8),
    "qb": ("sbuf", [128, 160], C8), "qs": ("sbuf", [128, 160], S8),
    "cb": ("sbuf", [128, 192], C8), "cs": ("sbuf", [128, 192], S8),
    "lp": ("sbuf", [128, 16], U), "ll": ("sbuf", [128, 16], U), "ofo": ("sbuf", [128, 8], U), "oc": ("sbuf", [128, 8], U),
    "offp": ("sbuf", [128, 32], U), "offl": ("sbuf", [128, 32], U),
    "ab": ("sbuf", [128, 256], F), "th": ("sbuf", [128, 256], F), "wt": ("sbuf", [128, 128], F),
    "sth": ("sbuf", [128, 8], F), "scb": ("sbuf", [128, 32], F),
    "cmp": ("sbuf", [128, 512], B), "rks": ("sbuf", [128, 256], B),
    "i32": ("sbuf", [128, 32], F), "coln": ("sbuf", [128, 2], B), "pi": ("sbuf", [128, 40], I), "pf": ("sbuf", [128, 16], F),
    "bi": ("sbuf", [128, 64], F), "k8": ("sbuf", [128, 256], B), "y8": ("sbuf", [128, 8], F), "ch8": ("sbuf", [128, 256], B),
    "vv": ("sbuf", [128, 128], B), "vt": ("sbuf", [128, 256], B), "sq": ("sbuf", [128, 128], B),
    "zt": ("sbuf", [128, 512], B),
    "lf": ("sbuf", [128, 32], F), "nt": ("sbuf", [128, 32], F), "nu": ("sbuf", [128, 32], F),
    "ent": ("sbuf", [128, 256], B), "m8": ("sbuf", [128, 2048], B), "rst": ("sbuf", [128, 2048], B), "mp": ("sbuf", [128, 2064], B),
    "pr": ("sbuf", [128, 256], B), "hp": ("sbuf", [128, 256], B), "hl": ("sbuf", [128, 256], B),
    "tv": ("sbuf", [128, 1040], F),
    "acb": ("sbuf", [128, 1024], F), "erb": ("sbuf", [128, 1024], F), "te": ("sbuf", [128, 128], F),
    "pa": ("psum", [128, 2048], F), "pb": ("psum", [128, 2048], F),
}
SEMAPHORES = ["v", "s", "t", "p", "dg1", "dg2", "du", "dl", "dh", "dm", "dsc", "dnb", "der", "dac", "l1", "l2", "c1", "s1", "a2", "b2",
              "sent", "left"]


def rank_program(g, core, T, topo):
    chip = topo.cores_of(core)
    ranks = [c for c in T.cores if c in chip]
    if not ranks:
        return
    others = [c for c in T.cores if c not in chip]
    peers = [c for c in others if topo.die(c) == topo.die(core)]
    helpers = [h for h in chip if h not in ranks and all(topo.may_write(h, c) for c in others)]
    aides = {c: min(a for a in chip if a not in ranks + helpers and topo.die(a) == topo.die(c)) for c in ranks}
    if core not in ranks + helpers + list(aides.values()):
        return

    def pair(c):
        return min(T.rank_of(d) for d in T.cores if d in topo.cores_of(c)) // 2

    me = pair(core)

    peers.sort(key=lambda c: (topo.same_plane(core, c), topo.mates(core, c)))

    def ids(cores):
        a = [topo.addr(c, core) for c in cores]
        return [DstId(rid=r_, pnc=p_) for r_, p_ in a]

    m2 = topo.mask(core, peers[2])
    n2 = bin(m2).count("1")
    b8 = dt.uint8

    def hop2(dst, src, local, sem, slots):
        g.remote_dma_fused([RemoteDMATransfer(dst_ids=ids([peers[i] for i in slots]), dma_engine_mask=m2, remote_sem=T.sem[sem],
                                              srcs=[src], dsts=[dst(i) for i in slots])], local_sem=T.sem[local])

    if core in helpers:
        g.wait_ge(T.sem.s1, sum(bin(topo.mask(c, core) & ~m2).count("1") for c in ranks))
        for sem, slots in (("a2", (0, 1)), ("b2", (2,))):
            hop2(lambda i: T.cs[:, 64 * i:64 * i + 64], T.qs[:, 0:64], "sent", sem, slots)
        g.wait_ge(T.sem.sent, 2 * n2)
        return
    if core not in ranks:
        src = [c for c in ranks if aides[c] == core][0]
        at = 128 + 32 * ranks.index(src)
        far = [c for c in others if topo.same_plane(core, c)]
        g.wait_ge(T.sem.c1, bin(topo.mask(src, core) & ~m2).count("1"))
        g.remote_dma_fused([RemoteDMATransfer(dst_ids=ids(far), dma_engine_mask=m2, remote_sem=T.sem.b2, srcs=[T.qb[:, 0:32].bitcast(b8)],
                                              dsts=[T.cb[:, at:at + 32].bitcast(b8) for c in far])], local_sem=T.sem.sent)
        g.wait_ge(T.sem.sent, n2)
        return

    rank = T.rank_of(core)
    partner = [c for c in ranks if c != core][0]
    first = rank < T.rank_of(partner)
    m1 = topo.mask(core, partner) & ~m2
    n1 = bin(m1).count("1")
    order = sorted(range(len(T.cores)), key=lambda s: (topo.die(T.cores[s]) != topo.die(T.cores[0]), s))
    at_l = order.index(rank)

    V, S, P, Y = g.vector, g.scalar, g.tensor, g.sync
    Q = {"v": V, "s": S, "t": P, "p": g, "y": Y}
    A, AF, X = AluOpType, ActivationFunctionType, AxisListType.X
    cnt, seen = {"sent": 0, "left": 0}, {}

    def done(sem, ins, n=1):
        ins.then_inc(T.sem[sem], n)
        cnt[sem] = cnt.get(sem, 0) + n
        return (sem, cnt[sem])

    def need(queue, *toks):
        for sem, n in toks:
            if seen.get((queue, sem), 0) < n:
                Q[queue].wait_ge(T.sem[sem], n)
                seen[(queue, sem)] = n

    q0 = 0 if first else 32
    own0 = 96 if first else 32
    pair0 = 96 if first else 0
    dec0 = 32 if first else 0
    far_c = 0 if first else 128

    d_u = done("du", S.dma_start(T.ub[:, 0:4], T.u[:, 0:4]), 16)
    d_1 = done("dg1", Y.dma_start(T.grb[:, 0:512], T.gr[:, 0:512]), 16)
    d_2 = done("dg2", Y.dma_start(T.grb[:, 512:1024], T.gr[:, 512:1024]), 16)

    def iota(buf, pattern, base, cm):
        return done("p", g.iota(buf, pattern, base, cm, allow_small_or_imprecise_dtypes=True))

    def tile_e(b):
        need("v", k_eb)
        return done("v", V.quantize_mx(T.eq[:, 128 * b:128 * b + 128], T.es[:, 128 * b:128 * b + 128], T.eb[:, 3 - b:515 - b]))

    done("v", V.memset(T.wt[:], PRED))
    k_eb = done("v", V.memset(T.eb[:], 0.0))
    k_p = done("p", g.iota(T.pi[:, 0:16], [[0, 16]], 0, 1))
    need("v", k_p)
    k_4 = done("v", V.tensor_scalar(T.pi[:, 16:32], T.pi[:, 0:16], 3, None, A.bitwise_and))
    k_i = iota(T.i32[:], [[1, 32]], 0, 0)
    need("p", k_eb)
    k_eb = done("p", g.affine_select(T.eb[:, 3:515:4], T.wt[:], [[-1, 128]], A.is_equal, 0.0, 0, 1))
    need("p", k_eb)
    k_wt = done("p", g.affine_select(T.wt[:], T.wt[:], [[-1, 128]], A.is_gt, 1.0, 0, 1))
    k_8 = iota(T.k8[:], [[0, 32], [1, 8]], 0, 0)
    iota(T.bi[:], [[16, 2], [0, 2], [1, 16]], 0, 0)
    k_c = iota(T.coln[:], [[1024, 2]], 0, 8)
    done("v", V.tensor_scalar(T.pi[:, 32:33], T.pi[:, 0:1], 1, None, A.bitwise_and))
    k = done("v", V.tensor_scalar(T.pi[:, 33:34], T.pi[:, 0:1], 1, 7, A.logical_shift_right, A.bitwise_and))
    need("v", k_4)
    k_uo = done("v", V.tensor_copy(T.uo[:], T.pi[:, 16:32]))
    k_zt = done("v", V.memset(T.zt[:], 0.0))
    need("v", k)
    done("v", V.tensor_copy(T.pf[:, 0:2], T.pi[:, 32:34]))
    p1, pq8, x8 = [T.pf[:, i:i + 1] for i in range(3)]
    tile_e(0)
    need("y", k_zt)
    d_h = done("dh", Y.dma_start(T.hb[:], T.zt[:]), 16)
    for a in range(4):
        d_m = done("dm", Y.dma_start(T.m8[:, 512 * a:512 * a + 512], T.zt[:]), 16)
    need("s", k_i)
    for a, s in enumerate(order):
        a_en = done("s", S.activation(T.ent[:, 32 * a:32 * a + 32], T.i32[:], AF.Copy, scale=2.0, bias=float(64 * s + 2)))

    need("s", d_u, k_uo)
    a_u = done("s", S.activation(T.urep[:, 256:512], T.ub[:, 0:4].indirect(T.uo[:, 0:16]), AF.Copy))
    for z in (T.tv[:, 0:2], T.tv[:, BB:BB + 2], T.mp[:, 0:1], T.lf[:]):
        done("s", S.activation(z, T.i32[:, 0:z.shape[1]], AF.Copy, scale=0.0))
    need("v", d_u, k_uo)
    k_u = done("v", V.tensor_copy(T.urep[:, 0:256], T.ub[:, 0:4].indirect(T.uo[:, 0:16])))

    a_c, a_f = [], []
    for h in range(2):
        j = 128 * h
        need("v", (d_1, d_2)[h])
        k_g = done("v", V.quantize_mx(T.gq[:, j:j + 128], T.gs[:, j:j + 128], T.grb[:, 512 * h:512 * h + 512]))
        if h == 0:
            need("v", k_u, a_u)
            k_u = done("v", V.quantize_mx(T.uq[:], T.us[:], T.urep[:]))
        need("t", k_u, k_g)
        t_c = done("t", P.matmul_mx(T.pa[:, 1024 * h:1024 * h + 128], T.gq[:, j:j + 128], T.gs[:, j:j + 128], T.uq[:], T.us[:], True, True))
        t_f = done("t", P.matmul_mx(T.pa[:, 1024 * h + 512:1024 * h + 640], T.uq[:], T.us[:], T.gq[:, j:j + 128], T.gs[:, j:j + 128], True, True))
        need("s", t_c)
        a_c.append(done("s", S.activation(T.sth[:, h:h + 1], T.pa[:, 1024 * h:1024 * h + 1], AF.Abs, bias=TINY)))
        need("s", t_f)
        a_f.append(done("s", S.activation(T.ab[:, j:j + 128], T.pa[:, 1024 * h + 512:1024 * h + 640], AF.Abs, bias=TINY)))
        if h == 0:
            tile_e(1)

    s0, s1 = T.sth[:, 0:1], T.sth[:, 1:2]
    need("s", k_wt, a_c[1])
    a_t = done("s", S.activation(T.th[:, 128:256], T.wt[:], AF.Copy, scale=s1))
    need("v", a_c[0], k_wt)
    k_d = done("v", V.tensor_scalar(T.th[:, 0:128], T.wt[:], s0, None, A.mult))
    need("v", a_f[0], k_d)
    done("v", V.tensor_tensor(T.cmp[:, 0:128], T.ab[:, 0:128], T.th[:, 0:128], A.is_gt))
    need("v", a_c[1])
    done("v", V.tensor_scalar(T.cmp[:, 256:384], T.ab[:, 0:128], s1, None, A.is_ge))
    need("v", a_f[1])
    k0 = done("v", V.tensor_scalar(T.cmp[:, 128:256], T.ab[:, 128:256], s0, None, A.is_gt))
    need("v", a_t)
    k1 = done("v", V.tensor_tensor(T.cmp[:, 384:512], T.ab[:, 128:256], T.th[:, 128:256], A.is_gt))
    need("v", k0)
    k0 = done("v", V.tensor_tensor_scan(T.rks[:, 0:128], T.cmp[:, 0:128], T.cmp[:, 128:256], 0.0, A.add, A.add))
    need("v", k1)
    k1 = done("v", V.tensor_tensor_scan(T.rks[:, 128:256], T.cmp[:, 256:384], T.cmp[:, 384:512], 0.0, A.add, A.add))
    rk = [T.rks[:, 127:128], T.rks[:, 255:256]]

    def resets(a, b):
        return [done("s", S.activation(T.rst[:, 256 * i:256 * i + 256], T.k8[:], AF.Sign)) for i in range(a, b)][-1]

    need("s", k_8)
    resets(0, 5)

    for h in range(2):
        need("v", k_c, (k0, k1)[h])
        for i in range(2):
            k = done("v", V.tensor_scalar(T.vv[:, 64 * i + 32 * h:64 * i + 32 * h + 32], T.bi[:, 32 * i:32 * i + 32], rk[h],
                                          T.coln[:, h:h + 1], A.is_equal, A.mult))
    tile_e(2)
    need("v", k)
    for a in range(2):
        k = done("v", V.transpose(T.vt[0:64, 128 * a:128 * a + 128], T.vv[64 * a:64 * a + 64, :]))
    k_e = tile_e(3)
    need("v", k)
    for i in range(2):
        k = done("v", V.tensor_tensor_scan(T.sq[0:64, 64 * i:64 * i + 64], T.vt[0:64, 64 * i:64 * i + 64],
                                           T.vt[0:64, 128 + 64 * i:192 + 64 * i], 0.0, A.add, A.add))
    done("v", V.tensor_scalar(T.y8[:], T.k8[:, 0:8], pq8, 1.0 / HOLD, A.is_le, A.max))
    done("v", V.tensor_scalar(T.ch8[:, 0:128], T.k8[:, 0:128], pq8, HOLD, A.is_gt, A.mult))
    need("v", k)
    for i in range(2):
        for a in range(4):
            k_lp = done("v", V.tensor_scalar(T.lp[32 * a:32 * a + 32, i:i + 1], T.sq[0:32, 64 * i + 63:64 * i + 64],
                                             T.sq[32:64, 64 * i + 63:64 * i + 64], float(rank), A.add, A.add))
    done("v", V.tensor_scalar(T.ch8[:, 128:256], T.k8[:, 128:256], pq8, HOLD, A.is_gt, A.mult))
    need("v", (k[0], k[1] + 1))
    done("v", V.tensor_reduce(x8, T.y8[:], X, A.mult))
    need("v", k_lp)
    k_o = [done("v", V.tensor_scalar(T.ofo[:, 2 * t:2 * t + 2], T.lp[:, 0:2], 0.5, t - rank / 2, A.mult, A.add)) for t in range(4)]
    h0 = 4 * (own0 - q0)
    k_oc = done("v", V.tensor_scalar(T.oc[:, 0:2], T.lp[:, 0:2], -float(rank), 0.125, A.add, A.mult))
    for t in range(4):
        q, dst, src = "ssvv"[t], T.hb[:, h0 + t:h0 + 128:4], T.grb[:, 0:1024].indirect(T.ofo[:, 2 * t:2 * t + 2])
        need(q, k_o[t], d_h)
        if q == "s":
            a_h = done("s", S.activation(dst, src, AF.Copy))
        else:
            k = done("v", V.tensor_copy(dst, src))
    need("v", k, a_h)
    k_q = done("v", V.quantize_mx(T.qb[:, q0:q0 + 128], T.qs[:, q0:q0 + 128], T.hb[:]))
    mine = T.ll[:, 2 * at_l:2 * at_l + 2]
    need("y", k_lp)
    d_l = done("dl", Y.dma_start(mine, T.lp[:, 0:2]), 16)

    L1, L2, C1, S1 = ("l1", len(peers) * n2), ("l2", n1 + (len(others) - len(peers)) * n2), ("c1", n1), ("s1", n1)
    A2, B2 = ("a2", 4 * n2), ("b2", 3 * n2)

    def lists(cores, mask, sem):
        return RemoteDMATransfer(dst_ids=ids(cores), dma_engine_mask=mask, remote_sem=T.sem[sem], srcs=[T.lp[:, 0:2]], dsts=[mine for c in cores])

    def hop1(cores, sem, src, dsts):
        g.remote_dma_fused([RemoteDMATransfer(dst_ids=ids(cores), dma_engine_mask=m1, remote_sem=T.sem[sem], srcs=[src], dsts=dsts)],
                           local_sem=T.sem.sent)

    need("p", k_lp)
    g.remote_dma_fused([lists(peers, m2, "l1")], local_sem=T.sem.sent)
    g.remote_dma_fused([lists([c for c in others if c not in peers], m2, "l2"), lists([partner], m1, "l2")], local_sem=T.sem.sent)
    need("p", k_q)
    hs = 0 if first else 32
    hop1(helpers, "s1", T.qs[:, own0:own0 + 32], [T.qs[:, hs:hs + 32] for h in helpers])
    hop1([aides[core], partner], "c1", T.qb[:, own0:own0 + 32].bitcast(b8), [T.qb[:, a:a + 32].bitcast(b8) for a in (0, far_c)])
    hop1([partner], "s1", T.qs[:, own0:own0 + 32], [T.qs[:, far_c:far_c + 32]])
    cnt["sent"] += 4 * n1 + 2 * n2
    need("p", C1)
    hop2(lambda i: T.cb[:, 64 * i:64 * i + 64].bitcast(b8), T.qb[:, pair0:pair0 + 64].bitcast(b8), "left", "a2", (0, 1))
    cnt["left"] += n2

    def decode(ps, codes, scales):
        return {b: done("t", P.matmul_mx(ps[:, 512 * b:512 * b + 128], T.eq[:, 128 * b:128 * b + 128], T.es[:, 128 * b:128 * b + 128],
                                         codes, scales, True, True)) for b in (0, 2, 1, 3)}

    need("t", k_e, a_f[1], k_q)
    td = decode(T.pa, T.qb[:, q0:q0 + 128], T.qs[:, q0:q0 + 128])
    a_e = done("s", S.activation(T.erb[:], T.grb[:], AF.Copy))
    need("s", k_oc, a_f[1])
    a_sc = done("s", S.activation(T.scb[:], T.ab[:, 0:256].indirect(T.oc[:, 0:2]), AF.Copy, bias=-TINY))
    a_r = resets(5, 8)
    for b in td:
        need("v", td[b])
        k_te = done("v", V.tensor_tensor(T.te[:, 32 * b:32 * b + 32], T.hb[:, h0 + b:h0 + 128:4],
                                         T.pa[:, 512 * b + own0 - q0:512 * b + own0 - q0 + 32], A.subtract))
    need("v", k_te, a_e)
    k_er = done("v", V.tensor_copy(T.erb[:, 0:1024].indirect(T.ofo[:, 0:8]), T.te[:]))
    need("y", a_sc)
    d_sc = done("dsc", Y.dma_start(T.sc[:], T.scb[0:1, :]), 16)
    need("y", k_er, ("left", n2))
    d_er = done("der", Y.dma_start(T.er[:], T.erb[:]), 16)

    got = {}

    def to_sum(q, tok, b, m, src):
        a = BB * (b % 2) + 2 + 128 * m + b // 2
        need(q, tok)
        dst = T.tv[:, a:a + 127:2]
        got.setdefault((b % 2, m), []).append(done(q, S.activation(dst, src, AF.Copy) if q == "s" else V.tensor_copy(dst, src)))

    need("t", C1, S1, k_te)
    td = decode(T.pa, T.qb[:, dec0:dec0 + 128], T.qs[:, dec0:dec0 + 128])
    for b in td:
        to_sum("s", td[b], b, me, T.pa[:, 512 * b + pair0 - dec0:512 * b + pair0 - dec0 + 64])

    def to_map(a):
        return done("v", V.tensor_copy(T.m8[:, 0:2048].indirect(T.ll[:, 8 * a:8 * a + 8]), T.ent[:, 128 * a:128 * a + 128]))

    need("v", L1, d_l, a_en, d_m)
    k = to_map(at_l // 4)
    need("v", k, L2)
    k = to_map(1 - at_l // 4)
    n = done("v", V.tensor_scalar(T.lf[0:32, 0:16], T.ll[0:32, 0:16], -3.5, 0.125, A.add, A.mult))
    need("v", k, a_r)
    k = done("v", V.tensor_tensor_scan(T.mp[:, 1:2049], T.rst[:], T.m8[:], 0.0, A.mult, A.max))
    need("v", n)
    n = done("v", V.transpose(T.nt[0:32, :], T.lf[0:32, :]))
    need("v", k)
    k = done("v", V.tensor_copy(T.pr[:, 0:224], T.mp[:, 0:2048].indirect(T.ll[:, 2:16])))
    k_hl = done("v", V.tensor_tensor_scan(T.hl[:], T.ch8[:], T.mp[:, 8:2049:8], 0.0, A.mult, A.add))
    need("v", k)
    k = done("v", V.tensor_tensor_scan(T.hp[:, 0:224], T.ch8[:, 0:224], T.pr[:, 0:224], 0.0, A.mult, A.add))
    need("v", n)
    k_nb = done("v", V.tensor_scalar(T.nu[0:32, :], T.nt[0:32, :], ROUND, ROUND, A.add, A.subtract))
    need("v", k)
    k_op = done("v", V.tensor_scalar(T.offp[:, 0:28], T.hp[:, 7:224:8], x8, p1, A.mult, A.add))
    need("y", k_nb)
    for a in range(2):
        d_nb = done("dnb", Y.dma_start(T.nb[order[4 * a]:8:2, :], T.nu[8 * a:8 * a + 8, 0:16]), 16)

    for tok, ps, c0, slots, qs in ((A2, T.pb, 0, (0, 1), "ssss"), (B2, T.pa, 64, (2,), "vsvs")):
        need("t", tok, *got[1, me])
        td = decode(ps, T.cb[:, c0:c0 + 128], T.cs[:, c0:c0 + 128])
        for b in td:
            for i in slots:
                to_sum(qs[b], td[b], b, pair(peers[i]), ps[:, 512 * b + 64 * i - c0:512 * b + 64 * i - c0 + 64])
    need("v", k_hl)
    k_ol = done("v", V.tensor_scalar(T.offl[:], T.hl[:, 7:256:8], x8, p1, A.mult, A.add))

    last = [None, None]
    for h, s in [(h, s) for s in range(1, 8) for h in range(2)]:
        o, own = 4 * order.index(s) - 4, T.tv[:, BB * h + 2 + 64 * s:BB * h + 66 + 64 * s]
        need("v", k_op, *got[h, s // 2], *got[h, 0])
        if last[h]:
            need("v", last[h])
        last[h] = done("v", V.tensor_tensor(own, T.tv[:, BB * h:BB * h + 2 + 64 * s].indirect(T.offp[:, o:o + 4]), own, A.add))

    need("s", k_ol, last[0])
    need("v", k_ol, last[1])
    for a, b in zip(PIECES, PIECES[1:]):
        off = T.offl[:, a // 32:b // 32]
        n = done("s", S.activation(T.acb[:, a:b:2], T.tv[:, 0:514].indirect(off), AF.Copy))
        k = done("v", V.tensor_copy(T.acb[:, a + 1:b:2], T.tv[:, BB:BB + 514].indirect(off)))
        need("y", k, n)
        d_ac = done("dac", Y.dma_start(T.acc[:, a:b], T.acb[:, a:b]), 16)

    need("p", d_u, d_1, d_2, d_h, d_m, d_l, d_er, d_nb, d_ac, d_sc, L1, L2, A2, B2)
    need("p", *[(x, cnt[x]) for x in ("v", "s", "t", "p", "sent", "left")])
